import numpy as np, ml_dtypes
CORES = [9,25,41,57]
N = 4
BF = ml_dtypes.bfloat16
def f(rng, *shape):
    return (rng.standard_normal(shape, dtype=np.float32) * np.exp2(rng.integers(-2, 3, shape[:-1] + (1,)))).astype(BF)
def wide(rng, *shape):
    v = f(rng, *shape).astype(np.float32); k = shape[:-2] + (1, shape[-1])
    return (v * np.exp2(rng.integers(-6, 7, k)) * (rng.random(k) > 0.0625)).astype(BF)
def gentries(a):
    return np.ascontiguousarray(a.reshape(8, 16, -1).transpose(0, 2, 1)).reshape(8, -1)
def gtable(e):
    e = np.asarray(e); return np.ascontiguousarray(e.reshape(8, -1, 16).transpose(0, 2, 1)).reshape(128, -1).astype(np.int32)
WAY = "abc"; W = len(WAY)
IC, CG, CAPP, TOT, S = 4096, 512, 1024, 4096, 512
def numbers(a):
    return np.stack([gentries(u) for u in a])
def slots(a):
    return np.stack([gentries(u) for u in a]).reshape(N, N, CAPP)
def columns(t, a):
    e = slots(a); t = t.astype(np.float64)
    return np.stack([np.concatenate([t[q][:, e[q, r]] for q in range(N)], axis=1) for r in range(N)])
def sums(t, x):
    return np.stack([np.bincount(x, weights=t[o], minlength=TOT) for o in range(16)])
def home(p, a):
    e = slots(a); y = np.zeros((N, 16, IC), np.float64)
    for q in range(N):
        for r in range(N):
            y[q][:, e[q, r]] += p[r][:, q * CAPP:(q + 1) * CAPP]
    return y
def anyslots(rng):
    return np.argsort(rng.random((W, N, N, IC)), axis=-1)[..., :CAPP]
def anynumbers(rng):
    x = rng.integers(0, TOT, (W, N, 8, S)); few = rng.integers(0, TOT, (W, N, 8, 32))
    return np.where(rng.random(x.shape) < 0.5, np.take_along_axis(few, rng.integers(0, 32, x.shape), axis=-1), x)
def make(rng, x, e):
    o = np.argsort(x[0], axis=-1, kind="stable"); x = np.stack([np.take_along_axis(u, o, axis=-1) for u in x])
    ob = np.lexsort((rng.random(x[1].shape), x[1]), axis=-1)
    d = {"f" + c: f(rng, N, 16, IC) for c in WAY}
    d["v"] = (rng.standard_normal((N, 8, S)) * np.exp2(rng.integers(-1, 2, (N, 8, 1)))).astype(np.float32)
    for w, c in enumerate(WAY): d["x" + c] = np.stack([gtable(u) for u in x[w]])
    d["ob"] = np.stack([gtable(u) for u in ob])
    for w, c in enumerate(WAY): d["l" + c] = np.stack([gtable(u.reshape(8, CG)) for u in e[w]])
    return d
def setup_inputs(rng):
    return make(rng, anynumbers(rng), anyslots(rng))
def setup_inputs_runs(rng):
    x = anynumbers(rng); h = rng.integers(0, TOT, (W, N, 8, 1))
    for w in range(W): x[w, :, :, w * S // 8:w * S // 8 + S // 2] = h[w]
    x[0, :, 0:2] = h[0, :, 0:1]; x[1, :, 1:3] = h[1, :, 1:2]
    return make(rng, x, anyslots(rng))
def setup_inputs_apart(rng):
    x = np.argsort(rng.random((W, N, 8 * S // TOT, TOT)), axis=-1).reshape(W, N, 8, S)
    return make(rng, x, anyslots(rng))
def setup_inputs_ends(rng):
    x = rng.integers(0, N, (W, N, 8, S)) * CAPP + rng.integers(0, 2, (W, N, 8, S)) * (CAPP - 1)
    x = np.where(rng.random(x.shape) < 0.75, x, rng.integers(0, TOT, x.shape)); x[..., 0] = 0; x[..., 1] = TOT - 1
    e = 1 + np.argsort(rng.random((W, N, N, IC - 2)), axis=-1)[..., :CAPP]; e[..., 0] = IC - 1; e[..., -1] = 0
    return make(rng, x, e)
def setup_inputs_alike(rng):
    x = anynumbers(rng); x[:, :, 1:] = x[:, :, :1].copy()
    e = np.repeat(np.argsort(rng.random((W, N, 1, IC)), axis=-1)[..., :CAPP], N, axis=2)
    return make(rng, x, e)
def setup_inputs_spread(rng):
    d = setup_inputs(rng)
    for c in WAY[1:]: d["f" + c] = wide(rng, N, 16, IC)
    return d
def check_inputs(d):
    bad = []
    for c in WAY:
        x = numbers(d["x" + c]); e = slots(d["l" + c])
        if not np.isfinite(d["f" + c].astype(np.float32)).all(): bad.append("finite_f" + c)
        if x.min() < 0 or x.max() >= TOT: bad.append("range_x" + c)
        if e.min() < 0 or e.max() >= IC: bad.append("range_l" + c)
        if (np.diff(np.sort(e, axis=-1), axis=-1) == 0).any(): bad.append("different_l" + c)
    if not np.isfinite(d["v"]).all(): bad.append("finite_v")
    if (np.diff(numbers(d["xa"]), axis=-1) < 0).any(): bad.append("sorted_xa")
    o = numbers(d["ob"])
    if not (np.sort(o, axis=-1) == np.arange(S)).all(): bad.append("places_ob")
    elif (np.diff(np.take_along_axis(numbers(d["xb"]), o, axis=-1), axis=-1) < 0).any(): bad.append("sorted_xb_by_ob")
    return bad
def reference(fa, fb, fc, v, xa, xb, xc, ob, la, lb, lc):
    xi = numbers(xa).reshape(N, 8 * S); xj = numbers(xb).reshape(N, 8 * S)
    w = np.repeat(v.astype(np.float64).reshape(N, 1, 8 * S), 16, axis=1)
    for t, x, a in ((fc, xc, lc),):
        u = columns(t, a); x = numbers(x).reshape(N, 8 * S)
        w = w * np.stack([u[r][:, x[r]] for r in range(N)])
    u = columns(fb, lb)
    ya = fa.astype(np.float64) * home([sums(w[r] * u[r][:, xj[r]], xi[r]) for r in range(N)], la)
    u = columns(ya, la)
    yb = home([sums(w[r] * u[r][:, xi[r]], xj[r]) for r in range(N)], lb)
    return {"ya": ya.astype(np.float32), "yb": yb.astype(np.float32)}

@@ -1,0 +1,461 @@
+from concourse.mybir import AluOpType, ActivationFunctionType
+
+OP = AluOpType
+COPY = ActivationFunctionType.Copy
+IDENTITY = ActivationFunctionType.Identity
+ZW = 4728
+HALF = 1024
+SIZES = {
+    "int32": {128: "Di Ei vsi vss", 4: "kri krs", 8: "kgi kgs k1 p15 hk", 32: "tla tlb txa txb txc tob ba bb bd pii bhi blo"},
+    "uint16": {32: "La Lb Lc ja jb jc jo pia pib snu offA offB bhu blu", 128: "idx inva invb", 256: "Lr"},
+    "bfloat16": {128: "E16", 4: "rsel", 512: "a1 a2 s1 s2 ssrc fag", 1024: "SELB CB LCB", 4096: "fcr fbr far Cw Bw W R",
+                 4096 - HALF: "fb16"},
+    "float32": {128: "E ident vsel N1 N2 m3", 4: "rm4", 8: "rm8 m0 m1 n0 hm hf hb", 32: "trash pif sn tr", 40: "yl", 64: "wlo whi m4",
+                256: "m2", 512: "X v8 vex vc xr mk w1 scn RT PT LP OT LA LQ faS ac0 ac1 ac2 ac3 yo", 520: "flA flB",
+                1024: "SEL", 1032: "pw0 pw1 pw2 pw3", 4096: "Aw", ZW: "zA zB"},
+}
+SCRATCH = {n: ("sbuf", [128, c], d) for d, x in SIZES.items() for c, names in x.items() for n in names.split()}
+for _t in ("la", "lb", "lc"):
+    SCRATCH["u" + _t] = ("sbuf", [128, 4, 8], "int32")
+SCRATCH["tm"] = ("sbuf", [128, 4, 4, 8], "float32")
+for _b in range(8):
+    SCRATCH["pb%d" % _b] = ("psum", [128, 512], "float32")
+ENG = {"v": "sv", "s": "ss", "t": "st", "g": "sg"}
+SEMAPHORES = (list(ENG.values()) + ["dt" + t for t in ("la", "lb", "xa", "xb", "xc", "ob")] + ["du" + t for t in ("la", "lb", "lc")]
+              + ["dv", "dfc", "dfb", "dfh", "dfa", "dfg", "dya", "dyb", "ls"]
+              + ["%s%d" % (k, d) for k in "cpnq" for d in (1, 2, 3)])
+
+
+def rank_program(g, core, T, topo):
+    me = T.rank_of(core)
+    if me is None:
+        return
+    N = len(T.cores)
+    queue = {"v": g.vector, "s": g.scalar, "t": g.tensor, "g": g, "y": g.sync}
+    count = {}
+    know = {e: {} for e in queue}
+    waited = {}
+    seen = {}
+    banks = {"pb%d" % b: {} for b in range(8)}
+
+    def wait(e, tok):
+        sem, val, _, kn = tok
+        if know[e].get(sem, 0) >= val:
+            return
+        queue[e].wait_ge(T.sem[sem], val)
+        waited[sem] = max(waited.get(sem, 0), val)
+        for k2, v2 in kn.items():
+            if know[e].get(k2, 0) < v2:
+                know[e][k2] = v2
+        know[e][sem] = val
+
+    def before(e, outs, ins):
+        for (_, n, lo, hi), w in [(x, True) for x in outs] + [(x, False) for x in ins]:
+            if n in banks:
+                for e2 in list(banks[n]):
+                    if e2 != e:
+                        wait(e, banks[n].pop(e2))
+                continue
+            for lo2, hi2, w2, tok in seen.get(n, []):
+                if lo2 < hi and lo < hi2 and (w or w2):
+                    wait(e, tok)
+
+    def after(outs, ins, tok):
+        for (_, n, lo, hi), w in [(x, True) for x in outs] + [(x, False) for x in ins]:
+            if n in banks:
+                banks[n][tok[2]] = tok
+                continue
+            old = seen.setdefault(n, [])
+            if w:
+                old[:] = [r for r in old if not (lo <= r[0] and r[1] <= hi)]
+            old.append((lo, hi, w, tok))
+
+    def emit(e, outs, ins, call):
+        before(e, outs, ins)
+        sem = ENG[e]
+        call(queue[e]).then_inc(T.sem[sem], 1)
+        count[sem] = count.get(sem, 0) + 1
+        after(outs, ins, (sem, count[sem], e, dict(know[e])))
+
+    def dmas(sem, items):
+        kn = {}
+        for e, o, i in items:
+            before(e, [o] if o[1] else [], [i] if i[1] else [])
+            queue[e].dma_start(out=o[0], in_=i[0]).then_inc(T.sem[sem], 16)
+            count[sem] = count.get(sem, 0) + 16
+            for k2, v2 in know[e].items():
+                kn[k2] = max(kn.get(k2, 0), v2)
+        tok = (sem, count[sem], "d", kn)
+        done = []
+        for e, o, i in items:
+            if o[1] and o[1:] not in done:
+                done.append(o[1:])
+                after([o], [], tok)
+            if i[1]:
+                after([], [i], tok)
+
+    def V(name, lo=0, hi=None, step=1, p0=0, p1=128):
+        if hi is None:
+            hi = SCRATCH[name][1][1]
+        ap = T[name][p0:p1, lo:hi] if step == 1 else T[name][p0:p1, lo:hi:step]
+        return (ap, name, lo, hi)
+
+    def H(ap):
+        return (ap, None, 0, 0)
+
+    turn = [0]
+
+    def bank():
+        turn[0] += 1
+        return "pb%d" % ((turn[0] - 1) % 8)
+
+    def ind(w, o):
+        return w[0].indirect(o[0])
+
+    def copy(o, i, e="v"):
+        if e == "v":
+            emit("v", [o], [i], lambda q: q.tensor_copy(o[0], i[0]))
+        else:
+            emit("s", [o], [i], lambda q: q.activation(o[0], i[0], COPY))
+
+    def scaled(o, i, sc, bias=None):
+        if bias is None:
+            emit("s", [o], [i, sc], lambda q: q.activation(o[0], i[0], COPY, scale=sc[0]))
+        else:
+            emit("s", [o], [i, sc, bias], lambda q: q.activation(o[0], i[0], IDENTITY, bias=bias[0], scale=sc[0]))
+
+    def ts(o, i, s1, op0, s2=None, op1=None):
+        rd = [i] + [s for s in (s1, s2) if isinstance(s, tuple)]
+        a1 = s1[0] if isinstance(s1, tuple) else s1
+        a2 = s2[0] if isinstance(s2, tuple) else s2
+        if op1 is None:
+            emit("v", [o], rd, lambda q: q.tensor_scalar(o[0], i[0], a1, None, op0))
+        else:
+            emit("v", [o], rd, lambda q: q.tensor_scalar(o[0], i[0], a1, a2, op0, op1))
+
+    def tt(o, a, b, op):
+        emit("v", [o], [a, b], lambda q: q.tensor_tensor(o[0], a[0], b[0], op))
+
+    def fill(o, x):
+        emit("v", [o], [], lambda q: q.memset(o[0], x))
+
+    def pick(o, w, l, e="v"):
+        if e == "v":
+            emit("v", [o], [w, l], lambda q: q.tensor_copy(o[0], ind(w, l)))
+        else:
+            emit("s", [o], [w, l], lambda q: q.activation(o[0], ind(w, l), COPY))
+
+    def pick2(o, w, l, b, op):
+        emit("v", [o], [w, l, b], lambda q: q.tensor_tensor(o[0], ind(w, l), b[0], op))
+
+    def put(w, l, i):
+        emit("v", [w], [l, i], lambda q: q.tensor_copy(ind(w, l), i[0]))
+
+    def mm(o, l, r, start=True, stop=True):
+        emit("t", [o], [l, r], lambda q: q.matmul(o[0], l[0], r[0], start, stop))
+
+    def iota(o, pattern, base, cm, small=False):
+        if small:
+            emit("g", [o], [], lambda q: q.iota(o[0], pattern, base, cm, allow_small_or_imprecise_dtypes=True))
+        else:
+            emit("g", [o], [], lambda q: q.iota(o[0], pattern, base, cm))
+
+    def send(q, src, dst, sem):
+        to = T.cores[q]
+        before("g", [], [src])
+        rid, pid, _ = topo.addr(to)
+        g.remote_dma(out_ap=dst, in_ap=src[0], remote_sem=T.sem["%s%d" % (sem, (q - me) % N)], local_sem=T.sem["ls"],
+                     pid=pid, routing_id=rid, dma_engine_mask=topo.mask(core, to))
+        count["ls"] = count.get("ls", 0) + len(topo.engines(core, to))
+
+    def expect(buf, width, sem):
+        for d in (1, 2, 3):
+            q, s = (me - d) % N, "%s%d" % (sem, d)
+            count[s] = len(topo.engines(T.cores[q], core))
+            after([V(buf, q * width, (q + 1) * width)], [], (s, count[s], "r", {}))
+
+    ring = [(me + d) % N for d in (1, 2, 3, 0)]
+    come = [(me - d) % N for d in (0, 1, 2, 3)]
+
+    def table(t, e):
+        dmas("dt" + t, [(e, V("t" + t), H(T[t][:, :]))])
+
+    def table3(t, e):
+        dmas("du" + t, [(e, (T["u" + t][:, :, :], "u" + t, 0, 32), H(T[t][:, :]))])
+
+    def group(name, b, lo=0, hi=None):
+        return V(name, lo, hi, p0=16 * b, p1=16 * b + 16)
+
+    table3("lc", "y")
+    dmas("dfh", [("s", V("fb16", p0=0, p1=16), H(T.fb[:, HALF:4096]))])
+    table3("lb", "s")
+    table("la", "y")
+    table("xa", "y")
+    dmas("dfc", [("y" if b < 4 else "s", group("fcr", b), H(T.fc[:, :])) for b in range(8)])
+    dmas("dfb", [("y", group("fbr", b, 0, HALF), H(T.fb[:, 0:HALF])) for b in range(8)])
+    table3("la", "y")
+    dmas("dv", [("y", V("v8", p0=0, p1=8), H(T.v[:, :]))])
+    for t in ("xc", "xb", "lb", "ob"):
+        table(t, "y")
+
+    iota(V("Di"), [[-1, 128]], 128, 1)
+    iota(V("k1"), [[0, 8]], 0, 1)
+    iota(V("kri"), [[-32, 4]], 0, 1)
+    iota(V("kgi"), [[-16, 8]], 0, 1)
+    iota(V("a1"), [[128, 4], [0, 128]], 0, 0, True)
+    iota(V("a2"), [[0, 4], [1, 128]], 8, 0, True)
+    iota(V("wlo"), [[1, 64]], 0, 0, True)
+    iota(V("trash"), [[16, 32]], 4097, 1, True)
+    iota(V("vsi", p1=8), [[1, 128]], 0, -16)
+    iota(V("whi"), [[64, 64]], 1, 0, True)
+
+    fill(V("X"), 0.0)
+    ts(V("Ei"), V("Di"), 15, OP.bitwise_and)
+    ts(V("hk"), V("k1"), 4, OP.arith_shift_right, 1, OP.bitwise_and)
+    ts(V("p15"), V("k1"), 15, OP.bitwise_and)
+    ts(V("krs"), V("kri"), 5, OP.arith_shift_right)
+    ts(V("kgs"), V("kgi"), 4, OP.arith_shift_right)
+    ts(V("E16"), V("Ei"), 0, OP.is_equal)
+    ts(V("E"), V("Ei"), 0, OP.is_equal)
+    ts(V("hf"), V("hk"), 1, OP.mult)
+    ts(V("m0"), V("p15"), 0, OP.is_equal)
+    ts(V("m1"), V("p15"), 1, OP.is_equal)
+    ts(V("hb"), V("hf"), 512.0, OP.mult, V("m0", 0, 1), OP.mult)
+    ts(V("rm4"), V("krs"), 0, OP.is_equal)
+    ts(V("hm"), V("hk"), 0, OP.is_equal)
+    for b in range(8):
+        ts(V("X", 128 * (b % 4) + 16 * b, 128 * (b % 4) + 16 * b + 16), V("E", 0, 16),
+           V("hm" if b < 4 else "hf", 0, 1), OP.mult)
+
+    def tiles_list(t):
+        u = (T["u" + t][:, :, :], "u" + t, 0, 32)
+        for r in range(4):
+            o, sc = (T["tm"][:, :, r, :], "tm", r, r + 1), V("rm4", r, r + 1)
+            emit("v", [o], [u, sc], lambda q: q.tensor_scalar(o[0], u[0], sc[0], None, OP.mult))
+        p = bank()
+        for b in range(4):
+            mm(V(p, 0, 32), V("X", 128 * b, 128 * b + 128), (T["tm"][:, b, :, :], "tm", 0, 4), b == 0, b == 3)
+        return p
+
+    scaled(V("s1"), V("a1"), V("m0", 0, 1), V("hb", 0, 1))
+    scaled(V("s2"), V("a2"), V("m1", 0, 1))
+    for i in range(HALF // 512, 8):
+        pb = bank()
+        mm(V(pb), V("E16", p1=16), V("fb16", 512 * i - HALF, 512 * i + 512 - HALF, p1=16))
+        copy(V("fbr", 512 * i, 512 * i + 512), V(pb), "s")
+    pc = tiles_list("lc")
+    ts(V("rm8"), V("kgs"), 0, OP.is_equal)
+    ts(V("n0"), V("p15"), 0, OP.not_equal)
+    copy(V("Lc"), V(pc, 0, 32))
+    pb = tiles_list("lb")
+    ts(V("N1"), V("Di"), 129, OP.is_equal, V("n0", 0, 1), OP.mult)
+    ts(V("N2"), V("Di"), 113, OP.is_equal, V("m0", 0, 1), OP.mult)
+    copy(V("Lb"), V(pb, 0, 32))
+    for name in ("SELB", "SEL"):
+        for b in range(8):
+            scaled(V(name, 128 * b, 128 * b + 128), V("E"), V("rm8", b, b + 1))
+
+    def places(t, dst):
+        ts(V("ba"), V(t), 0x1F0, OP.bitwise_and)
+        ts(V("bb"), V(t), 5, OP.arith_shift_right, 0x70, OP.bitwise_and)
+        ts(V("bd"), V(t), 15, OP.bitwise_and)
+        ts(V("ba"), V("ba"), 8, OP.mult)
+        tt(V("bb"), V("ba"), V("bb"), OP.add)
+        tt(V("pii"), V("bb"), V("bd"), OP.add)
+        copy(V(dst), V("pii"))
+
+    places("tla", "pia")
+    copy(V("pif"), V("pii"))
+    fill(V("yl"), 0.0)
+    ts(V("yl", 0, 32), V("txa"), 1, OP.add)
+    tt(V("ssrc"), V("s1"), V("s2"), OP.add)
+    ts(V("vss", p1=8), V("vsi", p1=8), 4, OP.arith_shift_right)
+    ts(V("vsel", p1=8), V("vss", p1=8), 0, OP.is_equal)
+
+    for r in ring:
+        pick(V("CB", 256 * r, 256 * r + 128), V("fcr"), V("Lc", 8 * r, 8 * r + 8))
+        pick(V("CB", 256 * r + 128, 256 * r + 256), V("fbr"), V("Lb", 8 * r, 8 * r + 8))
+        if r != me:
+            send(r, V("CB", 256 * r, 256 * r + 256), T["LCB"][:, 256 * me:256 * me + 256], "c")
+    expect("LCB", 256, "c")
+    iota(V("zA", 0, 4104), [[0, 4104]], 0, 0, True)
+
+    def runs(off, fl, e):
+        p = bank()
+        mm(V(p, 0, 32), V("N1"), V("yl", 0, 32), True, False)
+        mm(V(p, 0, 32), V("N2"), V("yl", 1, 33), False, True)
+        tt(V("sn"), V(p, 0, 32), V("yl", 0, 32), OP.is_equal)
+        copy(V("snu"), V("sn"))
+        tt(V("tr"), V("sn"), V("trash"), OP.mult)
+        tt(V("tr"), V("tr"), V("yl", 0, 32), OP.max)
+        copy(V(off), V("tr"))
+        fill(V(fl, 0, 8), 0.0)
+        pick(V(fl, 8, 520), V("wlo", 0, 8), V("snu"), e)
+
+    def lists(src, col):
+        p = bank()
+        for k in range(32):
+            mm(V(p, 4 * k, 4 * k + 4), V(src, 128 * col[k], 128 * col[k] + 128), V("rsel"))
+        return p
+
+    def unpack(dst, p):
+        for r in range(4):
+            copy(V(dst, 32 * r, 32 * r + 32), V(p, r, 128, 4))
+
+    pv = bank()
+    mm(V(pv), V("vsel", p1=8), V("v8", p1=8))
+    runs("offA", "flA", "s")
+    copy(V("vex"), V(pv), "s")
+    fill(V("W"), 0.0)
+    put(V("W"), V("pia"), V("ssrc"))
+    ts(V("rsel"), V("krs"), 0, OP.is_equal)
+
+    for n, q in enumerate(come):
+        buf = "CB" if q == me else "LCB"
+        if n == 2:
+            pl = bank()
+            for i in range(8):
+                mm(V(pl, 32 * i, 32 * i + 32), V("SEL", 128 * i, 128 * i + 128), V("pif"))
+            for k in range(8):
+                copy(V("Lr", 32 * k, 32 * k + 32), V(pl, k, 256, 8))
+            copy(V("jc"), V("txc"))
+            copy(V("jb"), V("txb"))
+        for f, win in ((0, "Cw"), (1, "Bw")):
+            for h in range(2):
+                pb = bank()
+                for b in range(4):
+                    mm(V(pb, 128 * b, 128 * b + 128), V("SELB", 128 * (4 * h + b), 128 * (4 * h + b) + 128),
+                       V(buf, 256 * q + 128 * f, 256 * q + 128 * f + 128))
+                copy(V(win, 1024 * q + 512 * h, 1024 * q + 512 * h + 512), V(pb),
+                     "s" if f == 1 and n == 3 else "sv"[h])
+    for rec in list(seen["LCB"]):
+        if rec[2]:
+            wait("y", rec[3])
+    dmas("dfa", [("y", group("far", b), H(T.fa[:, :])) for b in range(8)])
+    dmas("dfg", [("y", group("fag", b), H(T.fa[:, 512 * b:512 * b + 512])) for b in range(8)])
+    pia = lists("W", list(range(32)))
+    for i in range(4):
+        pick(V("R", 1024 * i, 1024 * i + 1024), V("W"), V("Lr", 64 * i, 64 * i + 64), "s")
+    pick2(V("vc"), V("Cw"), V("jc"), V("vex"), OP.mult)
+    pa = tiles_list("la")
+    pick2(V("w1"), V("Bw"), V("jb"), V("vc"), OP.mult)
+
+    def addruns(src, fl, off, z):
+        o, a, b = V("scn"), V(fl, 7, 519), V(src)
+        emit("v", [o], [a, b], lambda q: q.tensor_tensor_scan(o[0], a[0], b[0], 0.0, OP.mult, OP.add))
+        put(V(z), V(off), V("scn"))
+
+    def reduce(z, land, sem, e2, between):
+        p1, p2 = {}, {}
+
+        def sums(q):
+            p1[q] = bank()
+            for b in range(8):
+                c = 1 + 1024 * q + 128 * b
+                mm(V(p1[q], 16 * b, 16 * b + 16), V(z, c, c + 128), V("E", 0, 16))
+
+        sums(ring[0])
+        for j, q in enumerate(ring[:3]):
+            if j < 2:
+                sums(ring[j + 1])
+            copy(V("RT", 128 * q, 128 * q + 128), V(p1[q], 0, 128))
+            p2[q] = bank()
+            o, i, idn = V(p2[q], 0, 128), V("RT", 128 * q, 128 * q + 128), V("ident")
+            emit("t", [o], [i, idn], lambda k: k.transpose(o[0], i[0], idn[0]))
+            copy(V("PT", 128 * q, 128 * q + 128), V(p2[q], 0, 128), e2)
+            send(q, V("PT", 128 * q, 128 * q + 128), T[land][:, 128 * me:128 * me + 128], sem)
+        between()
+        for h in range(2):
+            p = bank()
+            c = 1 + 1024 * me + 512 * h
+            mm(V(p), V("E"), V(z, c, c + 512))
+            copy(V("pw%d" % me, 8 + 512 * h, 520 + 512 * h), V(p), "sv"[h])
+        expect(land, 128, sem)
+
+    def spread(buf, q, win, at, parts):
+        w = 8 // parts
+        for h in range(parts):
+            p = bank()
+            for b in range(w):
+                mm(V(p, 128 * b, 128 * b + 128), V("SEL", 128 * (w * h + b), 128 * (w * h + b) + 128),
+                   V(buf, 128 * q, 128 * q + 128))
+            copy(V(win, at + 128 * w * h, at + 128 * w * (h + 1)), V(p, 0, 128 * w), "sv"[h % 2])
+
+    ts(V("ident"), V("Di"), 128, OP.is_equal)
+    addruns("w1", "flA", "offA", "zA")
+    unpack("inva", pia)
+    copy(V("La"), V(pa, 0, 32))
+    reduce("zA", "LP", "p", "v", lambda: fill(V("W"), 0.0))
+    iota(V("zB", 0, 2048), [[0, 2048]], 0, 0, True)
+
+    def gather(q, lst, o, prev):
+        w, l = V("pw%d" % q), V(lst, 32 * q, 32 * q + 32)
+        if prev is None:
+            pick(V(o), w, l)
+        else:
+            pick2(V(o), w, l, V(prev), OP.add)
+
+    pi = lists("R", [(i % 8) * 4 + i // 8 for i in range(32)])
+    for r in range(4):
+        fill(V("pw%d" % r, 0, 8), 0.0)
+    ts(V("bhi"), V("txb"), 6, OP.arith_shift_right)
+    ts(V("blo"), V("txb"), 63, OP.bitwise_and)
+    copy(V("bhu"), V("bhi"))
+    copy(V("blu"), V("blo"))
+    unpack("idx", pi)
+    gather(me, "idx", "ac0", None)
+    pick(V("faS"), V("far"), V("La"), "s")
+    pick(V("yo"), V("wlo"), V("blu"), "s")
+    copy(V("jo"), V("tob"))
+    spread("LP", come[1], "pw%d" % come[1], 8, 2)
+    gather(come[1], "idx", "ac1", "ac0")
+    pick2(V("xr"), V("whi"), V("bhu"), V("yo"), OP.add)
+    spread("LP", come[2], "pw%d" % come[2], 8, 2)
+    gather(come[2], "idx", "ac2", "ac1")
+    places("tlb", "pib")
+    q = come[3]
+    spread("LP", q, "pw%d" % q, 8, 4)
+    for r in ring:
+        lo, hi = 128 * r, 128 * r + 128
+        pick2(V("ac3", lo, hi), V("pw%d" % q), V("idx", 32 * q + 8 * r, 32 * q + 8 * r + 8), V("ac2", lo, hi), OP.add)
+        tt(V("OT", lo, hi), V("ac3", lo, hi), V("faS", lo, hi), OP.mult)
+        if r != me:
+            send(r, V("OT", lo, hi), T["LA"][:, 128 * me:128 * me + 128], "n")
+    expect("LA", 128, "n")
+    iota(V("zB", 2048, 4104), [[0, 2056]], 0, 0, True)
+
+    spread("OT", me, "Aw", 1024 * me, 2)
+    for i in range(4):
+        pick2(V("mk", 128 * i, 128 * i + 128), V("xr"), V("jo", 8 * i, 8 * i + 8), V("E"), OP.mult)
+    tt(V("m2"), V("mk", 0, 512, 2), V("mk", 1, 512, 2), OP.add)
+    tt(V("m3"), V("m2", 0, 256, 2), V("m2", 1, 256, 2), OP.add)
+    tt(V("m4"), V("m3", 0, 128, 2), V("m3", 1, 128, 2), OP.add)
+    tt(V("yl", 0, 32), V("m4", 0, 64, 2), V("m4", 1, 64, 2), OP.add)
+    copy(V("ja"), V("txa"))
+
+    spread("LA", come[1], "Aw", 1024 * come[1], 2)
+    runs("offB", "flB", "s")
+    spread("LA", come[2], "Aw", 1024 * come[2], 2)
+    put(V("W"), V("pib"), V("ssrc"))
+    spread("LA", come[3], "Aw", 1024 * come[3], 4)
+    pib = lists("W", list(range(32)))
+    pick2(V("w1"), V("Aw"), V("ja"), V("vc"), OP.mult)
+    pick(V("mk"), V("w1"), V("jo"))
+    addruns("mk", "flB", "offB", "zB")
+    unpack("invb", pib)
+    reduce("zB", "LQ", "q", "s", lambda: gather(me, "inva", "ac0", None))
+    gather(come[1], "inva", "ac1", "ac0")
+    gather(come[2], "inva", "ac2", "ac1")
+    gather(come[3], "inva", "ac3", "ac2")
+    tt(V("yo"), V("ac3"), V("fag"), OP.mult)
+    dmas("dya", [("y", H(T.ya[:, 512 * b:512 * b + 512]), group("yo", b)) for b in range(8)])
+
+    gather(me, "invb", "ac0", None)
+    for i in (1, 2, 3):
+        q = come[i]
+        spread("LQ", q, "pw%d" % q, 8, 4 if i == 3 else 2)
+        gather(q, "invb", "ac%d" % i, "ac%d" % (i - 1))
+    dmas("dyb", [("ys"[b % 2], H(T.yb[:, 512 * b:512 * b + 512]), group("ac3", b)) for b in range(8)])
+    for sem, n in count.items():
+        if waited.get(sem, 0) < n:
+            g.wait_ge(T.sem[sem], n)

@@ -4,26 +4,155 @@ OP = AluOpType
 COPY = ActivationFunctionType.Copy
 IDENTITY = ActivationFunctionType.Identity
 ZW = 4728
-HALF = 1024
+DC = 2048
+OWN = 2
 SIZES = {
-    "int32": {128: "Di Ei vsi vss", 4: "kri krs", 8: "kgi kgs k1 p15 hk", 32: "tla tlb txa txb txc tob ba bb bd pii bhi blo"},
-    "uint16": {32: "La Lb Lc ja jb jc jo pia pib snu offA offB bhu blu", 128: "idx inva invb", 256: "Lr"},
-    "bfloat16": {128: "E16", 4: "rsel", 512: "a1 a2 s1 s2 ssrc fag", 1024: "SELB CB LCB", 4096: "fcr fbr far Cw Bw W R",
-                 4096 - HALF: "fb16"},
-    "float32": {128: "E ident vsel N1 N2 m3", 4: "rm4", 8: "rm8 m0 m1 n0 hm hf hb", 32: "trash pif sn tr", 40: "yl", 64: "wlo whi m4",
-                256: "m2", 512: "X v8 vex vc xr mk w1 scn RT PT LP OT LA LQ faS ac0 ac1 ac2 ac3 yo", 520: "flA flB",
-                1024: "SEL", 1032: "pw0 pw1 pw2 pw3", 4096: "Aw", ZW: "zA zB"},
+    "int32": {128: "Di Ei Gi Gs", 32: "tla tlb txa txb txc tob"},
+    "uint16": {256: "Lr"},
+    "bfloat16": {128: "E16", 512: "a1 a2 s1 s2 ssrc fag", 1024: "SELB CB LCB", 4096: "fcr fbr far Cw Bw W R fb16",
+                 4096 - DC: "fc16"},
+    "float32": {128: "E ident GRP vsel N1 N2 m3", 256: "m2", 520: "flA flB",
+                512: "X v8 vex vc vco xe xr mk w1 w2 scn scm RT PT RU PU LP OT LA LQ faS ac0 ac1 ac2 ac3 ya0 ya1 ya2 ya3 yo",
+                1024: "SEL", 1032: "pw0 pw1 pw2 pw3 qw", 4096: "Aw", ZW: "zA zB"},
+}
+SMALL = {
+    "int32": {4: "kri krs", 8: "kgi kgs k1 p15 hk", 32: "ba bb bd pii be bf bg pij nb nbi nhi nlo", 128: "vsi vss"},
+    "uint16": {32: "La Lb Lc ja jb jc jo pia pib snA snB offA offB", 128: "idx inva invb"},
+    "bfloat16": {4: "rsel"},
+    "float32": {4: "rm4", 8: "rm8 m0 m1 n0 hm hf hb w01", 32: "trash pif sa ta sb tb", 40: "yl ym", 64: "m4"},
 }
 SCRATCH = {n: ("sbuf", [128, c], d) for d, x in SIZES.items() for c, names in x.items() for n in names.split()}
+PLACE = {}
+for _d, _x in SMALL.items():
+    _at = 0
+    for _c, _names in _x.items():
+        for _n in _names.split():
+            PLACE[_n] = ("small_" + _d, _at, _c)
+            _at += -(-_c // 16) * 16
+    SCRATCH["small_" + _d] = ("sbuf", [128, _at], _d)
 for _t in ("la", "lb", "lc"):
     SCRATCH["u" + _t] = ("sbuf", [128, 4, 8], "int32")
-SCRATCH["tm"] = ("sbuf", [128, 4, 4, 8], "float32")
+    SCRATCH["tm" + _t[1]] = ("sbuf", [128, 4, 4, 8], "float32")
 for _b in range(8):
     SCRATCH["pb%d" % _b] = ("psum", [128, 512], "float32")
 ENG = {"v": "sv", "s": "ss", "t": "st", "g": "sg"}
 SEMAPHORES = (list(ENG.values()) + ["dt" + t for t in ("la", "lb", "xa", "xb", "xc", "ob")] + ["du" + t for t in ("la", "lb", "lc")]
-              + ["dv", "dfc", "dfb", "dfh", "dfa", "dfg", "dya", "dyb", "ls"]
+              + ["dv", "dfb", "dfc", "dfe", "dfa", "dfg", "dya", "dyb", "ls"]
               + ["%s%d" % (k, d) for k in "cpnq" for d in (1, 2, 3)])
+CYCLE, GATHER, SCATTER, WAKE, PE = 0.000913, 1.5, 3.2, 0.06, 0.5
+ISSUE, FIRST, HOP, RATE = 0.45, 1.0, 1.3, 55e3
+DMA_ISSUE, DMA_TIME, DMA_RATE = 0.07, 1.6, 180e3
+BYTES = {"float32": 4, "int32": 4, "bfloat16": 2, "uint16": 2}
+LEAN = {"list": 8.5, "inv": 5.0, "r": 0.6, "lb": 3.5, "vco": 2.0, "ib": 0.0, "ya": 0.0, "fas": 5.0, "own": 7.3, "wf": 0.0,
+        "ss": -2.5, "jc": -1.5, "vex": 0.0, "pw": 6.0, "red": 12.0}
+
+
+def op_time(op):
+    t = min(op["cost"].values()) if op["cost"] else 0.0
+    if op["kind"] == "send":
+        t += op["bytes"] / RATE + HOP
+    elif op["kind"] == "dma":
+        t += op["bytes"] / DMA_RATE + DMA_TIME
+    return t
+
+
+def order(ops):
+    n = len(ops)
+    pred = [set(op["after"]) for op in ops]
+    last = {}
+    for i, op in enumerate(ops):
+        both = [(v, True) for v in op["outs"] if v[0]] + [(v, False) for v in op["ins"] if v[0]]
+        for v, w in both:
+            for lo, hi, w2, j in last.setdefault(v[0], []):
+                if j != i and lo < v[2] and v[1] < hi and (w or w2):
+                    pred[i].add(j)
+        for v, w in both:
+            rec = last[v[0]]
+            if w:
+                rec[:] = [r for r in rec if not (v[1] <= r[0] and r[1] <= v[2])]
+            rec.append((v[1], v[2], w, i))
+    succ = [[] for _ in ops]
+    for i in range(n):
+        for j in pred[i]:
+            succ[j].append(i)
+    users = {}
+    for op in ops:
+        for b in op["banks"]:
+            users[b] = users.get(b, 0) + 1
+    prio = [0.0] * n
+    for i in reversed(range(n)):
+        prio[i] = op_time(ops[i]) + max([prio[k] + WAKE for k in succ[i]] or [0.0])
+    prio = [prio[i] + ops[i]["lean"] for i in range(n)]
+    free = {q: 0.0 for q in "vstgy"}
+    end = [None] * n
+    bank_of, bank_free = {}, {b: 0.0 for b in range(8)}
+    port, dma, first = 0.0, 0.0, True
+    out = []
+    ready = [i for i in range(n) if not pred[i]]
+    missing = [len(p) for p in pred]
+    chain = {}
+    for i, op in enumerate(ops):
+        if op["eng"] in "gy":
+            chain.setdefault(op["eng"], []).append(i)
+    while ready:
+        cand = []
+        for i in ready:
+            op = ops[i]
+            if op["eng"] in chain and chain[op["eng"]][0] != i:
+                continue
+            st = max([end[j] + WAKE for j in pred[i]] or [0.0])
+            bank = None
+            if op["eng"] == "t" and op["banks"] and op["banks"][0] not in bank_of:
+                idle = [b for b in bank_free if bank_free[b] is not None]
+                if not idle:
+                    continue
+                bank = min(idle, key=lambda b: bank_free[b])
+                st = max(st, bank_free[bank])
+            if op["eng"] == "-":
+                cand.append((st, i, "-", st, bank))
+                continue
+            best = None
+            for e in op["eng"]:
+                s1 = max(st, free[e])
+                f1 = s1 + op["cost"][e]
+                if best is None or f1 < best[0] - 0.01:
+                    best = (f1, i, e, s1, bank)
+            cand.append(best)
+        assert cand, "no call can go on"
+        f0, _, e0, _, _ = min(cand)
+        conflict = [c for c in cand if c[2] == e0 and c[3] < f0 - 1e-6] or [min(cand)]
+        f1, i, e, s1, bank = max(conflict, key=lambda c: (prio[c[1]], -c[1]))
+        op = ops[i]
+        ready.remove(i)
+        if op["eng"] in chain:
+            chain[op["eng"]].pop(0)
+        if bank is not None:
+            bank_of[op["banks"][0]] = bank
+            bank_free[bank] = None
+        end[i] = f1
+        if e != "-":
+            free[e] = f1
+        if op["kind"] == "dma":
+            dma = max(dma, f1) + op["bytes"] / DMA_RATE
+            end[i] = dma + DMA_TIME
+        elif op["kind"] == "send":
+            if first:
+                f1 += FIRST
+                first = False
+                free["g"] = f1
+            port = max(port, f1) + op["bytes"] / RATE
+            end[i] = port + HOP
+        for b in op["banks"]:
+            users[b] -= 1
+            if not users[b]:
+                bank_free[bank_of[b]] = f1 + WAKE
+        out.append((i, e, {b: "pb%d" % bank_of[b] for b in op["banks"]}))
+        for k in succ[i]:
+            missing[k] -= 1
+            if not missing[k]:
+                ready.append(k)
+    assert len(out) == n
+    return out
 
 
 def rank_program(g, core, T, topo):
@@ -37,6 +166,11 @@ def rank_program(g, core, T, topo):
     waited = {}
     seen = {}
     banks = {"pb%d" % b: {} for b in range(8)}
+    where = {}
+    ops = []
+    lean = [0.0]
+    turn = [0]
+    sent = {}
 
     def wait(e, tok):
         sem, val, _, kn = tok
@@ -50,7 +184,8 @@ def rank_program(g, core, T, topo):
         know[e][sem] = val
 
     def before(e, outs, ins):
-        for (_, n, lo, hi), w in [(x, True) for x in outs] + [(x, False) for x in ins]:
+        for (n, lo, hi, _), w in [(x, True) for x in outs] + [(x, False) for x in ins]:
+            n = where.get(n, n)
             if n in banks:
                 for e2 in list(banks[n]):
                     if e2 != e:
@@ -61,7 +196,8 @@ def rank_program(g, core, T, topo):
                     wait(e, tok)
 
     def after(outs, ins, tok):
-        for (_, n, lo, hi), w in [(x, True) for x in outs] + [(x, False) for x in ins]:
+        for (n, lo, hi, _), w in [(x, True) for x in outs] + [(x, False) for x in ins]:
+            n = where.get(n, n)
             if n in banks:
                 banks[n][tok[2]] = tok
                 continue
@@ -73,141 +209,204 @@ def rank_program(g, core, T, topo):
     def emit(e, outs, ins, call):
         before(e, outs, ins)
         sem = ENG[e]
-        call(queue[e]).then_inc(T.sem[sem], 1)
+        call(queue[e], e).then_inc(T.sem[sem], 1)
         count[sem] = count.get(sem, 0) + 1
         after(outs, ins, (sem, count[sem], e, dict(know[e])))
 
-    def dmas(sem, items):
+    def emit_dmas(sem, items, extra):
+        before(items[0][0], [], extra)
         kn = {}
         for e, o, i in items:
-            before(e, [o] if o[1] else [], [i] if i[1] else [])
-            queue[e].dma_start(out=o[0], in_=i[0]).then_inc(T.sem[sem], 16)
+            before(e, [o] if o[0] else [], [i] if i[0] else [])
+            queue[e].dma_start(out=o[3](), in_=i[3]()).then_inc(T.sem[sem], 16)
             count[sem] = count.get(sem, 0) + 16
             for k2, v2 in know[e].items():
                 kn[k2] = max(kn.get(k2, 0), v2)
         tok = (sem, count[sem], "d", kn)
         done = []
         for e, o, i in items:
-            if o[1] and o[1:] not in done:
-                done.append(o[1:])
+            if o[0] and o[:3] not in done:
+                done.append(o[:3])
                 after([o], [], tok)
-            if i[1]:
+            if i[0]:
                 after([], [i], tok)
 
-    def V(name, lo=0, hi=None, step=1, p0=0, p1=128):
-        if hi is None:
-            hi = SCRATCH[name][1][1]
-        ap = T[name][p0:p1, lo:hi] if step == 1 else T[name][p0:p1, lo:hi:step]
-        return (ap, name, lo, hi)
-
-    def H(ap):
-        return (ap, None, 0, 0)
-
-    turn = [0]
-
-    def bank():
-        turn[0] += 1
-        return "pb%d" % ((turn[0] - 1) % 8)
-
-    def ind(w, o):
-        return w[0].indirect(o[0])
-
-    def copy(o, i, e="v"):
-        if e == "v":
-            emit("v", [o], [i], lambda q: q.tensor_copy(o[0], i[0]))
-        else:
-            emit("s", [o], [i], lambda q: q.activation(o[0], i[0], COPY))
-
-    def scaled(o, i, sc, bias=None):
-        if bias is None:
-            emit("s", [o], [i, sc], lambda q: q.activation(o[0], i[0], COPY, scale=sc[0]))
-        else:
-            emit("s", [o], [i, sc, bias], lambda q: q.activation(o[0], i[0], IDENTITY, bias=bias[0], scale=sc[0]))
-
-    def ts(o, i, s1, op0, s2=None, op1=None):
-        rd = [i] + [s for s in (s1, s2) if isinstance(s, tuple)]
-        a1 = s1[0] if isinstance(s1, tuple) else s1
-        a2 = s2[0] if isinstance(s2, tuple) else s2
-        if op1 is None:
-            emit("v", [o], rd, lambda q: q.tensor_scalar(o[0], i[0], a1, None, op0))
-        else:
-            emit("v", [o], rd, lambda q: q.tensor_scalar(o[0], i[0], a1, a2, op0, op1))
-
-    def tt(o, a, b, op):
-        emit("v", [o], [a, b], lambda q: q.tensor_tensor(o[0], a[0], b[0], op))
-
-    def fill(o, x):
-        emit("v", [o], [], lambda q: q.memset(o[0], x))
-
-    def pick(o, w, l, e="v"):
-        if e == "v":
-            emit("v", [o], [w, l], lambda q: q.tensor_copy(o[0], ind(w, l)))
-        else:
-            emit("s", [o], [w, l], lambda q: q.activation(o[0], ind(w, l), COPY))
-
-    def pick2(o, w, l, b, op):
-        emit("v", [o], [w, l, b], lambda q: q.tensor_tensor(o[0], ind(w, l), b[0], op))
-
-    def put(w, l, i):
-        emit("v", [w], [l, i], lambda q: q.tensor_copy(ind(w, l), i[0]))
-
-    def mm(o, l, r, start=True, stop=True):
-        emit("t", [o], [l, r], lambda q: q.matmul(o[0], l[0], r[0], start, stop))
-
-    def iota(o, pattern, base, cm, small=False):
-        if small:
-            emit("g", [o], [], lambda q: q.iota(o[0], pattern, base, cm, allow_small_or_imprecise_dtypes=True))
-        else:
-            emit("g", [o], [], lambda q: q.iota(o[0], pattern, base, cm))
-
-    def send(q, src, dst, sem):
+    def emit_send(q, src, dst, sem):
         to = T.cores[q]
         before("g", [], [src])
         rid, pid, _ = topo.addr(to)
-        g.remote_dma(out_ap=dst, in_ap=src[0], remote_sem=T.sem["%s%d" % (sem, (q - me) % N)], local_sem=T.sem["ls"],
+        g.remote_dma(out_ap=dst, in_ap=src[3](), remote_sem=T.sem["%s%d" % (sem, (q - me) % N)], local_sem=T.sem["ls"],
                      pid=pid, routing_id=rid, dma_engine_mask=topo.mask(core, to))
         count["ls"] = count.get("ls", 0) + len(topo.engines(core, to))
 
-    def expect(buf, width, sem):
-        for d in (1, 2, 3):
-            q, s = (me - d) % N, "%s%d" % (sem, d)
-            count[s] = len(topo.engines(T.cores[q], core))
-            after([V(buf, q * width, (q + 1) * width)], [], (s, count[s], "r", {}))
+    def emit_come(v, s, q):
+        count[s] = len(topo.engines(T.cores[q], core))
+        after([v], [], (s, count[s], "r", {}))
 
-    ring = [(me + d) % N for d in (1, 2, 3, 0)]
-    come = [(me - d) % N for d in (0, 1, 2, 3)]
+    def V(name, lo=0, hi=None, step=1, p0=0, p1=128):
+        at = 0
+        if name in PLACE:
+            name, at, w = PLACE[name]
+            hi = w if hi is None else hi
+        elif hi is None:
+            hi = 512 if name[0] == "#" else SCRATCH[name][1][1]
+        lo, hi = lo + at, hi + at
 
-    def table(t, e):
-        dmas("dt" + t, [(e, V("t" + t), H(T[t][:, :]))])
+        def ap():
+            t = T[where.get(name, name)]
+            return t[p0:p1, lo:hi] if step == 1 else t[p0:p1, lo:hi:step]
+        return (name, lo, hi, ap)
 
-    def table3(t, e):
-        dmas("du" + t, [(e, (T["u" + t][:, :, :], "u" + t, 0, 32), H(T[t][:, :]))])
+    def H(ap):
+        return (None, 0, 0, lambda: ap)
 
     def group(name, b, lo=0, hi=None):
         return V(name, lo, hi, p0=16 * b, p1=16 * b + 16)
 
+    def bank():
+        turn[0] += 1
+        return "#%d" % turn[0]
+
+    def op(eng, outs, ins, subs, cost, kind="c", nbytes=0, needs=()):
+        names = []
+        for v in outs + ins:
+            if v[0] and v[0][0] == "#" and v[0] not in names:
+                names.append(v[0])
+        ops.append({"eng": eng, "outs": outs, "ins": ins, "subs": subs, "cost": cost, "kind": kind, "bytes": nbytes,
+                    "banks": names, "after": list(needs), "lean": lean[0]})
+        return len(ops) - 1
+
+    def size(v):
+        return v[2] - v[1]
+
+    def narrow(*vs):
+        return all(v[0][0] != "#" and BYTES[SCRATCH[v[0]][2]] == 2 for v in vs)
+
+    def cyc(n):
+        return max(64, n) * CYCLE
+
+    def one(eng, outs, ins, call, cost):
+        op(eng, outs, ins, [(outs, ins, call)], cost)
+
+    def copy(o, i, e="vs"):
+        n = size(o)
+        cost = {"v": cyc(n * 0.5 if narrow(o, i) else n), "s": cyc(n)}
+        one(e, [o], [i], lambda q, x: q.tensor_copy(o[3](), i[3]()) if x == "v" else q.activation(o[3](), i[3](), COPY), cost)
+
+    def scaled(o, i, sc, b=None):
+        if b is None:
+            one("s", [o], [i, sc], lambda q, x: q.activation(o[3](), i[3](), COPY, scale=sc[3]()), {"s": cyc(size(o))})
+        else:
+            one("s", [o], [i, sc, b], lambda q, x: q.activation(o[3](), i[3](), IDENTITY, bias=b[3](), scale=sc[3]()),
+                {"s": cyc(size(o))})
+
+    def ts(o, i, s1, op0, s2=None, op1=None, n=None):
+        rd = [i] + [s for s in (s1, s2) if isinstance(s, tuple)]
+
+        def call(q, x):
+            a1 = s1[3]() if isinstance(s1, tuple) else s1
+            a2 = s2[3]() if isinstance(s2, tuple) else s2
+            if op1 is None:
+                return q.tensor_scalar(o[3](), i[3](), a1, None, op0)
+            return q.tensor_scalar(o[3](), i[3](), a1, a2, op0, op1)
+        one("v", [o], rd, call, {"v": cyc(size(i))})
+
+    def tt(o, a, b, f):
+        n = size(a) * (1 if a[0][0] == "#" or b[0][0] == "#" else 2)
+        one("v", [o], [a, b], lambda q, x: q.tensor_tensor(o[3](), a[3](), b[3](), f), {"v": cyc(n)})
+
+    def fill(o, c):
+        one("v", [o], [], lambda q, x: q.memset(o[3](), c), {"v": cyc(size(o) * (0.5 if narrow(o) else 1))})
+
+    def ind(w, l):
+        return w[3]().indirect(l[3]())
+
+    def pick(o, w, l, e="vs"):
+        n = size(l) * 16 * GATHER * CYCLE
+        one(e, [o], [w, l], lambda q, x: q.tensor_copy(o[3](), ind(w, l)) if x == "v" else q.activation(o[3](), ind(w, l), COPY),
+            {"v": n + 0.05, "s": n + 0.065})
+
+    def pick2(o, w, l, b, f):
+        one("v", [o], [w, l, b], lambda q, x: q.tensor_tensor(o[3](), ind(w, l), b[3](), f),
+            {"v": size(l) * 16 * GATHER * CYCLE + 0.05})
+
+    def put(w, l, i):
+        one("v", [w], [l, i], lambda q, x: q.tensor_copy(ind(w, l), i[3]()), {"v": size(l) * 16 * SCATTER * CYCLE + 0.05})
+
+    def mms(items):
+        outs, ins, subs, cost = [], [], [], 0.0
+        for o, l, r, a, z in items:
+            outs.append(o)
+            ins += [l, r]
+            subs.append(([o], [l, r], lambda q, x, o=o, l=l, r=r, a=a, z=z: q.matmul(o[3](), l[3](), r[3](), a, z)))
+            cost += max(64, size(r)) * (1 if narrow(l) else 4) * PE * CYCLE
+        op("t", outs, ins, subs, {"t": cost})
+
+    def mm(o, l, r):
+        mms([(o, l, r, True, True)])
+
+    def iota(o, pattern, base, cm, small=False):
+        if small:
+            call = lambda q, x: q.iota(o[3](), pattern, base, cm, allow_small_or_imprecise_dtypes=True)
+        else:
+            call = lambda q, x: q.iota(o[3](), pattern, base, cm)
+        one("g", [o], [], call, {"g": 0.13 + 2 * size(o) * CYCLE})
+
+    def zeros(o):
+        iota(o, [[0, size(o)]], 0, 0, True)
+
+    def dmas(sem, items, nbytes, extra=()):
+        e = items[0][0]
+        outs, ins = [], list(extra)
+        for _, o, i in items:
+            outs += [o] if o[0] and o[:3] not in [x[:3] for x in outs] else []
+            ins += [i] if i[0] else []
+        op(e, outs, ins, (sem, items, list(extra)), {e: DMA_ISSUE * len(items)}, "dma", nbytes)
+
+    def send(q, src, dst, sem):
+        sent[sem, (q - me) % N] = op("g", [], [src], (q, src, dst, sem), {"g": ISSUE}, "send",
+                                     128 * size(src) * BYTES[SCRATCH[src[0]][2]])
+
+    def expect(buf, width, sem):
+        for d in (1, 2, 3):
+            q, s = (me - d) % N, "%s%d" % (sem, d)
+            v = V(buf, q * width, (q + 1) * width)
+            op("-", [v], [], (v, s, q), {}, "come", 0, [sent[sem, d]])
+
+    ring = [(me + d) % N for d in (1, 2, 3, 0)]
+    come = [(me - d) % N for d in (0, 1, 2, 3)]
+
+    def U(t):
+        return ("u" + t, 0, 32, lambda: T["u" + t][:, :, :])
+
+    def table(t, e):
+        dmas("dt" + t, [(e, V("t" + t), H(T[t][:, :]))], 16384)
+
+    def table3(t, e):
+        dmas("du" + t, [(e, U(t), H(T[t][:, :]))], 16384)
+
     table3("lc", "y")
-    dmas("dfh", [("s", V("fb16", p0=0, p1=16), H(T.fb[:, HALF:4096]))])
+    dmas("dfb", [("s", V("fb16", p0=0, p1=16), H(T.fb[:, :]))], 131072)
+    dmas("dfe", [("y", V("fc16", p0=0, p1=16), H(T.fc[:, DC:4096]))], 65536)
     table3("lb", "s")
+    dmas("dfc", [("y", group("fcr", b, 0, DC), H(T.fc[:, 0:DC])) for b in range(8)], 16 * DC * 2 * 8)
     table("la", "y")
     table("xa", "y")
-    dmas("dfc", [("y" if b < 4 else "s", group("fcr", b), H(T.fc[:, :])) for b in range(8)])
-    dmas("dfb", [("y", group("fbr", b, 0, HALF), H(T.fb[:, 0:HALF])) for b in range(8)])
     table3("la", "y")
-    dmas("dv", [("y", V("v8", p0=0, p1=8), H(T.v[:, :]))])
-    for t in ("xc", "xb", "lb", "ob"):
+    dmas("dv", [("y", V("v8", p0=0, p1=8), H(T.v[:, :]))], 16384)
+    for t in ("xc", "xb", "ob", "lb"):
         table(t, "y")
 
     iota(V("Di"), [[-1, 128]], 128, 1)
     iota(V("k1"), [[0, 8]], 0, 1)
     iota(V("kri"), [[-32, 4]], 0, 1)
     iota(V("kgi"), [[-16, 8]], 0, 1)
+    iota(V("trash"), [[16, 32]], 4097, 1, True)
+    iota(V("w01"), [[1, 8]], 0, 0, True)
+    iota(V("vsi", p1=8), [[1, 128]], 0, -16)
+    iota(V("Gi"), [[-16, 8], [0, 16]], 0, 1)
     iota(V("a1"), [[128, 4], [0, 128]], 0, 0, True)
     iota(V("a2"), [[0, 4], [1, 128]], 8, 0, True)
-    iota(V("wlo"), [[1, 64]], 0, 0, True)
-    iota(V("trash"), [[16, 32]], 4097, 1, True)
-    iota(V("vsi", p1=8), [[1, 128]], 0, -16)
-    iota(V("whi"), [[64, 64]], 1, 0, True)
 
     fill(V("X"), 0.0)
     ts(V("Ei"), V("Di"), 15, OP.bitwise_and)
@@ -226,51 +425,34 @@ def rank_program(g, core, T, topo):
     for b in range(8):
         ts(V("X", 128 * (b % 4) + 16 * b, 128 * (b % 4) + 16 * b + 16), V("E", 0, 16),
            V("hm" if b < 4 else "hf", 0, 1), OP.mult)
-
-    def tiles_list(t):
-        u = (T["u" + t][:, :, :], "u" + t, 0, 32)
-        for r in range(4):
-            o, sc = (T["tm"][:, :, r, :], "tm", r, r + 1), V("rm4", r, r + 1)
-            emit("v", [o], [u, sc], lambda q: q.tensor_scalar(o[0], u[0], sc[0], None, OP.mult))
-        p = bank()
-        for b in range(4):
-            mm(V(p, 0, 32), V("X", 128 * b, 128 * b + 128), (T["tm"][:, b, :, :], "tm", 0, 4), b == 0, b == 3)
-        return p
-
-    scaled(V("s1"), V("a1"), V("m0", 0, 1), V("hb", 0, 1))
-    scaled(V("s2"), V("a2"), V("m1", 0, 1))
-    for i in range(HALF // 512, 8):
-        pb = bank()
-        mm(V(pb), V("E16", p1=16), V("fb16", 512 * i - HALF, 512 * i + 512 - HALF, p1=16))
-        copy(V("fbr", 512 * i, 512 * i + 512), V(pb), "s")
-    pc = tiles_list("lc")
     ts(V("rm8"), V("kgs"), 0, OP.is_equal)
     ts(V("n0"), V("p15"), 0, OP.not_equal)
-    copy(V("Lc"), V(pc, 0, 32))
-    pb = tiles_list("lb")
     ts(V("N1"), V("Di"), 129, OP.is_equal, V("n0", 0, 1), OP.mult)
     ts(V("N2"), V("Di"), 113, OP.is_equal, V("m0", 0, 1), OP.mult)
-    copy(V("Lb"), V(pb, 0, 32))
-    for name in ("SELB", "SEL"):
-        for b in range(8):
-            scaled(V(name, 128 * b, 128 * b + 128), V("E"), V("rm8", b, b + 1))
-
-    def places(t, dst):
-        ts(V("ba"), V(t), 0x1F0, OP.bitwise_and)
-        ts(V("bb"), V(t), 5, OP.arith_shift_right, 0x70, OP.bitwise_and)
-        ts(V("bd"), V(t), 15, OP.bitwise_and)
-        ts(V("ba"), V("ba"), 8, OP.mult)
-        tt(V("bb"), V("ba"), V("bb"), OP.add)
-        tt(V("pii"), V("bb"), V("bd"), OP.add)
-        copy(V(dst), V("pii"))
-
-    places("tla", "pia")
-    copy(V("pif"), V("pii"))
-    fill(V("yl"), 0.0)
-    ts(V("yl", 0, 32), V("txa"), 1, OP.add)
-    tt(V("ssrc"), V("s1"), V("s2"), OP.add)
+    ts(V("ident"), V("Di"), 128, OP.is_equal)
+    ts(V("rsel"), V("krs"), 0, OP.is_equal)
+    ts(V("Gs"), V("Gi"), 4, OP.arith_shift_right)
+    ts(V("GRP"), V("Gs"), 0, OP.is_equal)
     ts(V("vss", p1=8), V("vsi", p1=8), 4, OP.arith_shift_right)
     ts(V("vsel", p1=8), V("vss", p1=8), 0, OP.is_equal)
+
+    def tiles_list(t, dst):
+        tm, u = "tm" + t[1], U(t)
+        for r in range(4):
+            ts((tm, r, r + 1, lambda r=r: T[tm][:, :, r, :]), u, V("rm4", r, r + 1), OP.mult)
+        p = bank()
+        mms([(V(p, 0, 32), V("X", 128 * b, 128 * b + 128), (tm, 0, 4, lambda b=b: T[tm][:, b, :, :]), b == 0, b == 3)
+             for b in range(4)])
+        copy(V(dst), V(p, 0, 32), "v")
+
+    tiles_list("lc", "Lc")
+    tiles_list("lb", "Lb")
+    for i in range(8):
+        for src, dst, lo in (("fc16", "fcr", DC), ("fb16", "fbr", 0)):
+            if 512 * i >= lo:
+                p = bank()
+                mm(V(p), V("E16", p1=16), V(src, 512 * i - lo, 512 * i - lo + 512, p1=16))
+                copy(V(dst, 512 * i, 512 * i + 512), V(p))
 
     for r in ring:
         pick(V("CB", 256 * r, 256 * r + 128), V("fcr"), V("Lc", 8 * r, 8 * r + 8))
@@ -278,184 +460,222 @@ def rank_program(g, core, T, topo):
         if r != me:
             send(r, V("CB", 256 * r, 256 * r + 256), T["LCB"][:, 256 * me:256 * me + 256], "c")
     expect("LCB", 256, "c")
-    iota(V("zA", 0, 4104), [[0, 4104]], 0, 0, True)
+    for i in range(4):
+        zeros(V("zA", 1026 * i, 1026 * i + 1026))
 
-    def runs(off, fl, e):
+    dmas("dfa", [("y", group("far", b), H(T.fa[:, :])) for b in range(8)], 1 << 20, [V("LCB")])
+    dmas("dfg", [("y", group("fag", b), H(T.fa[:, 512 * b:512 * b + 512])) for b in range(8)], 131072)
+
+    for name in ("SELB", "SEL"):
+        for b in range(8):
+            scaled(V(name, 128 * b, 128 * b + 128), V("E"), V("rm8", b, b + 1))
+    lean[0] = LEAN["ss"]
+    scaled(V("s1"), V("a1"), V("m0", 0, 1), V("hb", 0, 1))
+    scaled(V("s2"), V("a2"), V("m1", 0, 1))
+    tt(V("ssrc"), V("s1"), V("s2"), OP.add)
+
+    def places(t, dst, a, b, d, e):
+        ts(V(a), V(t), 0x1F0, OP.bitwise_and)
+        ts(V(b), V(t), 5, OP.arith_shift_right, 0x70, OP.bitwise_and)
+        ts(V(d), V(t), 15, OP.bitwise_and)
+        ts(V(a), V(a), 8, OP.mult)
+        tt(V(b), V(a), V(b), OP.add)
+        tt(V(e), V(b), V(d), OP.add)
+        copy(V(dst), V(e), "v")
+
+    def runs(yl, sn, tr, snu, off, fl):
         p = bank()
-        mm(V(p, 0, 32), V("N1"), V("yl", 0, 32), True, False)
-        mm(V(p, 0, 32), V("N2"), V("yl", 1, 33), False, True)
-        tt(V("sn"), V(p, 0, 32), V("yl", 0, 32), OP.is_equal)
-        copy(V("snu"), V("sn"))
-        tt(V("tr"), V("sn"), V("trash"), OP.mult)
-        tt(V("tr"), V("tr"), V("yl", 0, 32), OP.max)
-        copy(V(off), V("tr"))
+        mms([(V(p, 0, 32), V("N1"), V(yl, 0, 32), True, False), (V(p, 0, 32), V("N2"), V(yl, 1, 33), False, True)])
+        tt(V(sn), V(p, 0, 32), V(yl, 0, 32), OP.is_equal)
+        copy(V(snu), V(sn), "v")
+        tt(V(tr), V(sn), V("trash"), OP.mult)
+        tt(V(tr), V(tr), V(yl, 0, 32), OP.max)
+        copy(V(off), V(tr), "v")
         fill(V(fl, 0, 8), 0.0)
-        pick(V(fl, 8, 520), V("wlo", 0, 8), V("snu"), e)
+        pick(V(fl, 8, 520), V("w01"), V(snu))
 
-    def lists(src, col):
+    def lists(src, col, dst):
         p = bank()
-        for k in range(32):
-            mm(V(p, 4 * k, 4 * k + 4), V(src, 128 * col[k], 128 * col[k] + 128), V("rsel"))
-        return p
-
-    def unpack(dst, p):
+        mms([(V(p, 4 * k, 4 * k + 4), V(src, 128 * col[k], 128 * col[k] + 128), V("rsel"), True, True) for k in range(32)])
         for r in range(4):
-            copy(V(dst, 32 * r, 32 * r + 32), V(p, r, 128, 4))
+            copy(V(dst, 32 * r, 32 * r + 32), V(p, r, 128, 4), "v")
 
-    pv = bank()
-    mm(V(pv), V("vsel", p1=8), V("v8", p1=8))
-    runs("offA", "flA", "s")
-    copy(V("vex"), V(pv), "s")
-    fill(V("W"), 0.0)
+    lean[0] = LEAN["vex"]
+    p = bank()
+    mm(V(p), V("vsel", p1=8), V("v8", p1=8))
+    copy(V("vex"), V(p))
+    lean[0] = LEAN["list"]
+    fill(V("yl"), 0.0)
+    ts(V("yl", 0, 32), V("txa"), 1, OP.add)
+    runs("yl", "sa", "ta", "snA", "offA", "flA")
+    lean[0] = LEAN["jc"]
+    copy(V("jc"), V("txc"), "v")
+    copy(V("jb"), V("txb"), "v")
+    lean[0] = LEAN["fas"]
+    tiles_list("la", "La")
+    lean[0] = LEAN["inv"]
+    places("tla", "pia", "ba", "bb", "bd", "pii")
+    copy(V("pif"), V("pii"), "v")
+    lean[0] = LEAN["wf"]
+    for i in range(4):
+        fill(V("W", 1024 * i, 1024 * i + 1024), 0.0)
+    lean[0] = LEAN["inv"]
     put(V("W"), V("pia"), V("ssrc"))
-    ts(V("rsel"), V("krs"), 0, OP.is_equal)
+    p = bank()
+    mms([(V(p, 32 * i, 32 * i + 32), V("SEL", 128 * i, 128 * i + 128), V("pif"), True, True) for i in range(8)])
+    for k in range(8):
+        copy(V("Lr", 32 * k, 32 * k + 32), V(p, k, 256, 8), "v")
+    lean[0] = LEAN["r"]
+    for i in range(8):
+        pick(V("R", 512 * i, 512 * i + 512), V("W"), V("Lr", 32 * i, 32 * i + 32), "s")
+    lists("R", [(i % 8) * 4 + i // 8 for i in range(32)], "idx")
+    lean[0] = LEAN["ya"]
+    lists("W", list(range(32)), "inva")
+    lean[0] = 0.0
 
     for n, q in enumerate(come):
         buf = "CB" if q == me else "LCB"
-        if n == 2:
-            pl = bank()
-            for i in range(8):
-                mm(V(pl, 32 * i, 32 * i + 32), V("SEL", 128 * i, 128 * i + 128), V("pif"))
-            for k in range(8):
-                copy(V("Lr", 32 * k, 32 * k + 32), V(pl, k, 256, 8))
-            copy(V("jc"), V("txc"))
-            copy(V("jb"), V("txb"))
         for f, win in ((0, "Cw"), (1, "Bw")):
             for h in range(2):
-                pb = bank()
-                for b in range(4):
-                    mm(V(pb, 128 * b, 128 * b + 128), V("SELB", 128 * (4 * h + b), 128 * (4 * h + b) + 128),
-                       V(buf, 256 * q + 128 * f, 256 * q + 128 * f + 128))
-                copy(V(win, 1024 * q + 512 * h, 1024 * q + 512 * h + 512), V(pb),
-                     "s" if f == 1 and n == 3 else "sv"[h])
-    for rec in list(seen["LCB"]):
-        if rec[2]:
-            wait("y", rec[3])
-    dmas("dfa", [("y", group("far", b), H(T.fa[:, :])) for b in range(8)])
-    dmas("dfg", [("y", group("fag", b), H(T.fa[:, 512 * b:512 * b + 512])) for b in range(8)])
-    pia = lists("W", list(range(32)))
-    for i in range(4):
-        pick(V("R", 1024 * i, 1024 * i + 1024), V("W"), V("Lr", 64 * i, 64 * i + 64), "s")
+                p = bank()
+                mms([(V(p, 128 * b, 128 * b + 128), V("SELB", 128 * (4 * h + b), 128 * (4 * h + b) + 128),
+                      V(buf, 256 * q + 128 * f, 256 * q + 128 * f + 128), True, True) for b in range(4)])
+                copy(V(win, 1024 * q + 512 * h, 1024 * q + 512 * h + 512), V(p))
     pick2(V("vc"), V("Cw"), V("jc"), V("vex"), OP.mult)
-    pa = tiles_list("la")
     pick2(V("w1"), V("Bw"), V("jb"), V("vc"), OP.mult)
 
-    def addruns(src, fl, off, z):
-        o, a, b = V("scn"), V(fl, 7, 519), V(src)
-        emit("v", [o], [a, b], lambda q: q.tensor_tensor_scan(o[0], a[0], b[0], 0.0, OP.mult, OP.add))
-        put(V(z), V(off), V("scn"))
+    def addruns(src, fl, off, z, scn):
+        o, a, b = V(scn), V(fl, 7, 519), V(src)
+        one("v", [o], [a, b], lambda q, x: q.tensor_tensor_scan(o[3](), a[3](), b[3](), 0.0, OP.mult, OP.add), {"v": cyc(512)})
+        put(V(z), V(off), V(scn))
 
-    def reduce(z, land, sem, e2, between):
-        p1, p2 = {}, {}
-
-        def sums(q):
-            p1[q] = bank()
-            for b in range(8):
-                c = 1 + 1024 * q + 128 * b
-                mm(V(p1[q], 16 * b, 16 * b + 16), V(z, c, c + 128), V("E", 0, 16))
-
-        sums(ring[0])
-        for j, q in enumerate(ring[:3]):
-            if j < 2:
-                sums(ring[j + 1])
-            copy(V("RT", 128 * q, 128 * q + 128), V(p1[q], 0, 128))
-            p2[q] = bank()
-            o, i, idn = V(p2[q], 0, 128), V("RT", 128 * q, 128 * q + 128), V("ident")
-            emit("t", [o], [i, idn], lambda k: k.transpose(o[0], i[0], idn[0]))
-            copy(V("PT", 128 * q, 128 * q + 128), V(p2[q], 0, 128), e2)
-            send(q, V("PT", 128 * q, 128 * q + 128), T[land][:, 128 * me:128 * me + 128], sem)
-        between()
-        for h in range(2):
+    def reduce(z, land, sem, RT, PT, pw):
+        lean[0] = LEAN["red"]
+        for q in ring[:3]:
             p = bank()
-            c = 1 + 1024 * me + 512 * h
-            mm(V(p), V("E"), V(z, c, c + 512))
-            copy(V("pw%d" % me, 8 + 512 * h, 520 + 512 * h), V(p), "sv"[h])
+            mms([(V(p, 16 * b, 16 * b + 16), V(z, 1 + 1024 * q + 128 * b, 129 + 1024 * q + 128 * b), V("E", 0, 16), True, True)
+                 for b in range(8)])
+            copy(V(RT, 128 * q, 128 * q + 128), V(p, 0, 128))
+            p = bank()
+            o, i, idn = V(p, 0, 128), V(RT, 128 * q, 128 * q + 128), V("ident")
+            op("t", [o], [i, idn], [([o], [i, idn], lambda k, x, o=o, i=i: k.transpose(o[3](), i[3](), idn[3]()))],
+               {"t": 512 * PE * CYCLE})
+            copy(V(PT, 128 * q, 128 * q + 128), V(p, 0, 128))
+            send(q, V(PT, 128 * q, 128 * q + 128), T[land][:, 128 * me:128 * me + 128], sem)
+        lean[0] = LEAN["pw"]
+        for h in range(4):
+            p = bank()
+            c = 1 + 1024 * me + 256 * h
+            mm(V(p, 0, 256), V("E"), V(z, c, c + 256))
+            copy(V(pw, 8 + 256 * h, 264 + 256 * h), V(p, 0, 256))
+        lean[0] = 0.0
         expect(land, 128, sem)
 
     def spread(buf, q, win, at, parts):
         w = 8 // parts
         for h in range(parts):
             p = bank()
-            for b in range(w):
-                mm(V(p, 128 * b, 128 * b + 128), V("SEL", 128 * (w * h + b), 128 * (w * h + b) + 128),
-                   V(buf, 128 * q, 128 * q + 128))
-            copy(V(win, at + 128 * w * h, at + 128 * w * (h + 1)), V(p, 0, 128 * w), "sv"[h % 2])
+            mms([(V(p, 128 * b, 128 * b + 128), V("SEL", 128 * (w * h + b), 128 * (w * h + b) + 128),
+                  V(buf, 128 * q, 128 * q + 128), True, True) for b in range(w)])
+            copy(V(win, at + 128 * w * h, at + 128 * w * (h + 1)), V(p, 0, 128 * w))
 
-    ts(V("ident"), V("Di"), 128, OP.is_equal)
-    addruns("w1", "flA", "offA", "zA")
-    unpack("inva", pia)
-    copy(V("La"), V(pa, 0, 32))
-    reduce("zA", "LP", "p", "v", lambda: fill(V("W"), 0.0))
-    iota(V("zB", 0, 2048), [[0, 2048]], 0, 0, True)
+    addruns("w1", "flA", "offA", "zA", "scn")
+    zeros(V("fcr", 0, 2048))
+    reduce("zA", "LP", "p", "RT", "PT", "pw%d" % me)
 
-    def gather(q, lst, o, prev):
-        w, l = V("pw%d" % q), V(lst, 32 * q, 32 * q + 32)
+    def gather(q, lst, o, prev, own="pw%d" % me):
+        w, l = V(own if q == me else "pw%d" % q), V(lst, 32 * q, 32 * q + 32)
         if prev is None:
             pick(V(o), w, l)
         else:
             pick2(V(o), w, l, V(prev), OP.add)
 
-    pi = lists("R", [(i % 8) * 4 + i // 8 for i in range(32)])
-    for r in range(4):
-        fill(V("pw%d" % r, 0, 8), 0.0)
-    ts(V("bhi"), V("txb"), 6, OP.arith_shift_right)
-    ts(V("blo"), V("txb"), 63, OP.bitwise_and)
-    copy(V("bhu"), V("bhi"))
-    copy(V("blu"), V("blo"))
-    unpack("idx", pi)
+    zeros(V("fcr", 2048, 4096))
+    zeros(V("zB", 0, 2048))
+    for name in ("qw", "pw0", "pw1", "pw2", "pw3"):
+        fill(V(name, 0, 8), 0.0)
     gather(me, "idx", "ac0", None)
-    pick(V("faS"), V("far"), V("La"), "s")
-    pick(V("yo"), V("wlo"), V("blu"), "s")
-    copy(V("jo"), V("tob"))
-    spread("LP", come[1], "pw%d" % come[1], 8, 2)
-    gather(come[1], "idx", "ac1", "ac0")
-    pick2(V("xr"), V("whi"), V("bhu"), V("yo"), OP.add)
-    spread("LP", come[2], "pw%d" % come[2], 8, 2)
-    gather(come[2], "idx", "ac2", "ac1")
-    places("tlb", "pib")
+    lean[0] = LEAN["fas"]
+    pick(V("faS"), V("far"), V("La"))
+    lean[0] = 0.0
+    for n in (1, 2):
+        spread("LP", come[n], "pw%d" % come[n], 8, 4)
+        gather(come[n], "idx", "ac%d" % n, "ac%d" % (n - 1))
     q = come[3]
-    spread("LP", q, "pw%d" % q, 8, 4)
-    for r in ring:
+    spread("LP", q, "pw%d" % q, 8, 8)
+    for r in ring[:OWN] + [me] + ring[OWN:3]:
         lo, hi = 128 * r, 128 * r + 128
+        lean[0] = LEAN["own"] if r == me else 0.0
         pick2(V("ac3", lo, hi), V("pw%d" % q), V("idx", 32 * q + 8 * r, 32 * q + 8 * r + 8), V("ac2", lo, hi), OP.add)
         tt(V("OT", lo, hi), V("ac3", lo, hi), V("faS", lo, hi), OP.mult)
         if r != me:
             send(r, V("OT", lo, hi), T["LA"][:, 128 * me:128 * me + 128], "n")
+    lean[0] = 0.0
     expect("LA", 128, "n")
-    iota(V("zB", 2048, 4104), [[0, 2056]], 0, 0, True)
+    zeros(V("zB", 2048, 4104))
 
-    spread("OT", me, "Aw", 1024 * me, 2)
+    lean[0] = LEAN["lb"]
+    ts(V("nb"), V("txb"), 4096, OP.mult)
+    tt(V("nbi"), V("nb"), V("txa"), OP.add)
+    for k in range(16):
+        ts(("xe", k, k + 1, lambda k=k: T["xe"][:, k:512:16]), V("nbi"), V("E", k, k + 1), OP.mult)
+    p = bank()
+    mm(V(p), V("GRP"), V("xe"))
+    copy(V("xr"), V(p))
+    copy(V("jo"), V("tob"), "v")
     for i in range(4):
         pick2(V("mk", 128 * i, 128 * i + 128), V("xr"), V("jo", 8 * i, 8 * i + 8), V("E"), OP.mult)
     tt(V("m2"), V("mk", 0, 512, 2), V("mk", 1, 512, 2), OP.add)
     tt(V("m3"), V("m2", 0, 256, 2), V("m2", 1, 256, 2), OP.add)
     tt(V("m4"), V("m3", 0, 128, 2), V("m3", 1, 128, 2), OP.add)
-    tt(V("yl", 0, 32), V("m4", 0, 64, 2), V("m4", 1, 64, 2), OP.add)
-    copy(V("ja"), V("txa"))
+    tt(V("nhi"), V("m4", 0, 64, 2), V("m4", 1, 64, 2), OP.add)
+    ts(V("nlo"), V("nhi"), 4095, OP.bitwise_and)
+    copy(V("ja"), V("nlo"), "v")
+    ts(V("nhi"), V("nhi"), 12, OP.arith_shift_right)
+    fill(V("ym"), 0.0)
+    ts(V("ym", 0, 32), V("nhi"), 1, OP.add)
+    runs("ym", "sb", "tb", "snB", "offB", "flB")
+    lean[0] = LEAN["vco"]
+    pick(V("vco"), V("vc"), V("jo"))
+    lean[0] = LEAN["ib"]
+    places("tlb", "pib", "be", "bf", "bg", "pij")
+    put(V("fcr"), V("pib"), V("ssrc"))
+    lists("fcr", list(range(32)), "invb")
 
-    spread("LA", come[1], "Aw", 1024 * come[1], 2)
-    runs("offB", "flB", "s")
-    spread("LA", come[2], "Aw", 1024 * come[2], 2)
-    put(V("W"), V("pib"), V("ssrc"))
-    spread("LA", come[3], "Aw", 1024 * come[3], 4)
-    pib = lists("W", list(range(32)))
-    pick2(V("w1"), V("Aw"), V("ja"), V("vc"), OP.mult)
-    pick(V("mk"), V("w1"), V("jo"))
-    addruns("mk", "flB", "offB", "zB")
-    unpack("invb", pib)
-    reduce("zB", "LQ", "q", "s", lambda: gather(me, "inva", "ac0", None))
-    gather(come[1], "inva", "ac1", "ac0")
-    gather(come[2], "inva", "ac2", "ac1")
-    gather(come[3], "inva", "ac3", "ac2")
-    tt(V("yo"), V("ac3"), V("fag"), OP.mult)
-    dmas("dya", [("y", H(T.ya[:, 512 * b:512 * b + 512]), group("yo", b)) for b in range(8)])
+    lean[0] = LEAN["ya"]
+    gather(me, "inva", "ya0", None)
+    for n in (1, 2, 3):
+        gather(come[n], "inva", "ya%d" % n, "ya%d" % (n - 1))
+    tt(V("yo"), V("ya3"), V("fag"), OP.mult)
+    dmas("dya", [("y", H(T.ya[:, 512 * b:512 * b + 512]), group("yo", b)) for b in range(8)], 262144)
+    lean[0] = 0.0
 
-    gather(me, "invb", "ac0", None)
-    for i in (1, 2, 3):
-        q = come[i]
-        spread("LQ", q, "pw%d" % q, 8, 4 if i == 3 else 2)
-        gather(q, "invb", "ac%d" % i, "ac%d" % (i - 1))
-    dmas("dyb", [("ys"[b % 2], H(T.yb[:, 512 * b:512 * b + 512]), group("ac3", b)) for b in range(8)])
+    spread("OT", me, "Aw", 1024 * me, 4)
+    for n in (1, 2, 3):
+        spread("LA", come[n], "Aw", 1024 * come[n], 4)
+    pick2(V("w2"), V("Aw"), V("ja"), V("vco"), OP.mult)
+    addruns("w2", "flB", "offB", "zB", "scm")
+    reduce("zB", "LQ", "q", "RU", "PU", "qw")
+
+    gather(me, "invb", "ac0", None, "qw")
+    for n in (1, 2, 3):
+        q = come[n]
+        spread("LQ", q, "pw%d" % q, 8, 4)
+        gather(q, "invb", "ac%d" % n, "ac%d" % (n - 1))
+    dmas("dyb", [("ys"[b % 2], H(T.yb[:, 512 * b:512 * b + 512]), group("ac3", b)) for b in range(8)], 262144)
+
+    for i, e, at in order(ops):
+        where.update(at)
+        o = ops[i]
+        if o["kind"] == "c":
+            for outs, ins, call in o["subs"]:
+                emit(e, outs, ins, call)
+        elif o["kind"] == "dma":
+            emit_dmas(*o["subs"])
+        elif o["kind"] == "send":
+            emit_send(*o["subs"])
+        else:
+            emit_come(*o["subs"])
     for sem, n in count.items():
         if waited.get(sem, 0) < n:
             g.wait_ge(T.sem[sem], n)

from concourse.mybir import AluOpType, ActivationFunctionType

OP = AluOpType
COPY = ActivationFunctionType.Copy
IDENTITY = ActivationFunctionType.Identity
ZW = 4728
DC = 2048
OWN = 2
SIZES = {
    "int32": {128: "Di Ei Gi Gs", 32: "tla tlb txa txb txc tob"},
    "uint16": {256: "Lr"},
    "bfloat16": {128: "E16", 512: "a1 a2 s1 s2 ssrc fag", 1024: "SELB CB LCB", 4096: "fcr fbr far Cw Bw W R fb16",
                 4096 - DC: "fc16"},
    "float32": {128: "E ident GRP vsel N1 N2 m3", 256: "m2", 520: "flA flB",
                512: "X v8 vex vc vco xe xr mk w1 w2 scn scm RT PT RU PU LP OT LA LQ faS ac0 ac1 ac2 ac3 ya0 ya1 ya2 ya3 yo",
                1024: "SEL", 1032: "pw0 pw1 pw2 pw3 qw", 4096: "Aw", ZW: "zA zB"},
}
SMALL = {
    "int32": {4: "kri krs", 8: "kgi kgs k1 p15 hk", 32: "ba bb bd pii be bf bg pij nb nbi nhi nlo", 128: "vsi vss"},
    "uint16": {32: "La Lb Lc ja jb jc jo pia pib snA snB offA offB", 128: "idx inva invb"},
    "bfloat16": {4: "rsel"},
    "float32": {4: "rm4", 8: "rm8 m0 m1 n0 hm hf hb w01", 32: "trash pif sa ta sb tb", 40: "yl ym", 64: "m4"},
}
SCRATCH = {n: ("sbuf", [128, c], d) for d, x in SIZES.items() for c, names in x.items() for n in names.split()}
PLACE = {}
for _d, _x in SMALL.items():
    _at = 0
    for _c, _names in _x.items():
        for _n in _names.split():
            PLACE[_n] = ("small_" + _d, _at, _c)
            _at += -(-_c // 16) * 16
    SCRATCH["small_" + _d] = ("sbuf", [128, _at], _d)
for _t in ("la", "lb", "lc"):
    SCRATCH["u" + _t] = ("sbuf", [128, 4, 8], "int32")
    SCRATCH["tm" + _t[1]] = ("sbuf", [128, 4, 4, 8], "float32")
for _b in range(8):
    SCRATCH["pb%d" % _b] = ("psum", [128, 512], "float32")
ENG = {"v": "sv", "s": "ss", "t": "st", "g": "sg"}
SEMAPHORES = (list(ENG.values()) + ["dt" + t for t in ("la", "lb", "xa", "xb", "xc", "ob")] + ["du" + t for t in ("la", "lb", "lc")]
              + ["dv", "dfb", "dfc", "dfe", "dfa", "dfg", "dya", "dyb", "ls"]
              + ["%s%d" % (k, d) for k in "cpnq" for d in (1, 2, 3)])
CYCLE, GATHER, SCATTER, WAKE, PE = 0.000913, 1.5, 3.2, 0.06, 0.5
ISSUE, FIRST, HOP, RATE = 0.45, 1.0, 1.3, 55e3
DMA_ISSUE, DMA_TIME, DMA_RATE = 0.07, 1.6, 180e3
BYTES = {"float32": 4, "int32": 4, "bfloat16": 2, "uint16": 2}
LEAN = {"list": 8.5, "inv": 5.0, "r": 0.6, "lb": 3.5, "vco": 2.0, "ib": 0.0, "ya": 0.0, "fas": 5.0, "own": 7.3, "wf": 0.0,
        "ss": -2.5, "jc": -1.5, "vex": 0.0, "pw": 6.0, "red": 12.0}


def op_time(op):
    t = min(op["cost"].values()) if op["cost"] else 0.0
    if op["kind"] == "send":
        t += op["bytes"] / RATE + HOP
    elif op["kind"] == "dma":
        t += op["bytes"] / DMA_RATE + DMA_TIME
    return t


def order(ops):
    n = len(ops)
    pred = [set(op["after"]) for op in ops]
    last = {}
    for i, op in enumerate(ops):
        both = [(v, True) for v in op["outs"] if v[0]] + [(v, False) for v in op["ins"] if v[0]]
        for v, w in both:
            for lo, hi, w2, j in last.setdefault(v[0], []):
                if j != i and lo < v[2] and v[1] < hi and (w or w2):
                    pred[i].add(j)
        for v, w in both:
            rec = last[v[0]]
            if w:
                rec[:] = [r for r in rec if not (v[1] <= r[0] and r[1] <= v[2])]
            rec.append((v[1], v[2], w, i))
    succ = [[] for _ in ops]
    for i in range(n):
        for j in pred[i]:
            succ[j].append(i)
    users = {}
    for op in ops:
        for b in op["banks"]:
            users[b] = users.get(b, 0) + 1
    prio = [0.0] * n
    for i in reversed(range(n)):
        prio[i] = op_time(ops[i]) + max([prio[k] + WAKE for k in succ[i]] or [0.0])
    prio = [prio[i] + ops[i]["lean"] for i in range(n)]
    free = {q: 0.0 for q in "vstgy"}
    end = [None] * n
    bank_of, bank_free = {}, {b: 0.0 for b in range(8)}
    port, dma, first = 0.0, 0.0, True
    out = []
    ready = [i for i in range(n) if not pred[i]]
    missing = [len(p) for p in pred]
    chain = {}
    for i, op in enumerate(ops):
        if op["eng"] in "gy":
            chain.setdefault(op["eng"], []).append(i)
    while ready:
        cand = []
        for i in ready:
            op = ops[i]
            if op["eng"] in chain and chain[op["eng"]][0] != i:
                continue
            st = max([end[j] + WAKE for j in pred[i]] or [0.0])
            bank = None
            if op["eng"] == "t" and op["banks"] and op["banks"][0] not in bank_of:
                idle = [b for b in bank_free if bank_free[b] is not None]
                if not idle:
                    continue
                bank = min(idle, key=lambda b: bank_free[b])
                st = max(st, bank_free[bank])
            if op["eng"] == "-":
                cand.append((st, i, "-", st, bank))
                continue
            best = None
            for e in op["eng"]:
                s1 = max(st, free[e])
                f1 = s1 + op["cost"][e]
                if best is None or f1 < best[0] - 0.01:
                    best = (f1, i, e, s1, bank)
            cand.append(best)
        assert cand, "no call can go on"
        f0, _, e0, _, _ = min(cand)
        conflict = [c for c in cand if c[2] == e0 and c[3] < f0 - 1e-6] or [min(cand)]
        f1, i, e, s1, bank = max(conflict, key=lambda c: (prio[c[1]], -c[1]))
        op = ops[i]
        ready.remove(i)
        if op["eng"] in chain:
            chain[op["eng"]].pop(0)
        if bank is not None:
            bank_of[op["banks"][0]] = bank
            bank_free[bank] = None
        end[i] = f1
        if e != "-":
            free[e] = f1
        if op["kind"] == "dma":
            dma = max(dma, f1) + op["bytes"] / DMA_RATE
            end[i] = dma + DMA_TIME
        elif op["kind"] == "send":
            if first:
                f1 += FIRST
                first = False
                free["g"] = f1
            port = max(port, f1) + op["bytes"] / RATE
            end[i] = port + HOP
        for b in op["banks"]:
            users[b] -= 1
            if not users[b]:
                bank_free[bank_of[b]] = f1 + WAKE
        out.append((i, e, {b: "pb%d" % bank_of[b] for b in op["banks"]}))
        for k in succ[i]:
            missing[k] -= 1
            if not missing[k]:
                ready.append(k)
    assert len(out) == n
    return out


def rank_program(g, core, T, topo):
    me = T.rank_of(core)
    if me is None:
        return
    N = len(T.cores)
    queue = {"v": g.vector, "s": g.scalar, "t": g.tensor, "g": g, "y": g.sync}
    count = {}
    know = {e: {} for e in queue}
    waited = {}
    seen = {}
    banks = {"pb%d" % b: {} for b in range(8)}
    where = {}
    ops = []
    lean = [0.0]
    turn = [0]
    sent = {}

    def wait(e, tok):
        sem, val, _, kn = tok
        if know[e].get(sem, 0) >= val:
            return
        queue[e].wait_ge(T.sem[sem], val)
        waited[sem] = max(waited.get(sem, 0), val)
        for k2, v2 in kn.items():
            if know[e].get(k2, 0) < v2:
                know[e][k2] = v2
        know[e][sem] = val

    def before(e, outs, ins):
        for (n, lo, hi, _), w in [(x, True) for x in outs] + [(x, False) for x in ins]:
            n = where.get(n, n)
            if n in banks:
                for e2 in list(banks[n]):
                    if e2 != e:
                        wait(e, banks[n].pop(e2))
                continue
            for lo2, hi2, w2, tok in seen.get(n, []):
                if lo2 < hi and lo < hi2 and (w or w2):
                    wait(e, tok)

    def after(outs, ins, tok):
        for (n, lo, hi, _), w in [(x, True) for x in outs] + [(x, False) for x in ins]:
            n = where.get(n, n)
            if n in banks:
                banks[n][tok[2]] = tok
                continue
            old = seen.setdefault(n, [])
            if w:
                old[:] = [r for r in old if not (lo <= r[0] and r[1] <= hi)]
            old.append((lo, hi, w, tok))

    def emit(e, outs, ins, call):
        before(e, outs, ins)
        sem = ENG[e]
        call(queue[e], e).then_inc(T.sem[sem], 1)
        count[sem] = count.get(sem, 0) + 1
        after(outs, ins, (sem, count[sem], e, dict(know[e])))

    def emit_dmas(sem, items, extra):
        before(items[0][0], [], extra)
        kn = {}
        for e, o, i in items:
            before(e, [o] if o[0] else [], [i] if i[0] else [])
            queue[e].dma_start(out=o[3](), in_=i[3]()).then_inc(T.sem[sem], 16)
            count[sem] = count.get(sem, 0) + 16
            for k2, v2 in know[e].items():
                kn[k2] = max(kn.get(k2, 0), v2)
        tok = (sem, count[sem], "d", kn)
        done = []
        for e, o, i in items:
            if o[0] and o[:3] not in done:
                done.append(o[:3])
                after([o], [], tok)
            if i[0]:
                after([], [i], tok)

    def emit_send(q, src, dst, sem):
        to = T.cores[q]
        before("g", [], [src])
        rid, pid, _ = topo.addr(to)
        g.remote_dma(out_ap=dst, in_ap=src[3](), remote_sem=T.sem["%s%d" % (sem, (q - me) % N)], local_sem=T.sem["ls"],
                     pid=pid, routing_id=rid, dma_engine_mask=topo.mask(core, to))
        count["ls"] = count.get("ls", 0) + len(topo.engines(core, to))

    def emit_come(v, s, q):
        count[s] = len(topo.engines(T.cores[q], core))
        after([v], [], (s, count[s], "r", {}))

    def V(name, lo=0, hi=None, step=1, p0=0, p1=128):
        at = 0
        if name in PLACE:
            name, at, w = PLACE[name]
            hi = w if hi is None else hi
        elif hi is None:
            hi = 512 if name[0] == "#" else SCRATCH[name][1][1]
        lo, hi = lo + at, hi + at

        def ap():
            t = T[where.get(name, name)]
            return t[p0:p1, lo:hi] if step == 1 else t[p0:p1, lo:hi:step]
        return (name, lo, hi, ap)

    def H(ap):
        return (None, 0, 0, lambda: ap)

    def group(name, b, lo=0, hi=None):
        return V(name, lo, hi, p0=16 * b, p1=16 * b + 16)

    def bank():
        turn[0] += 1
        return "#%d" % turn[0]

    def op(eng, outs, ins, subs, cost, kind="c", nbytes=0, needs=()):
        names = []
        for v in outs + ins:
            if v[0] and v[0][0] == "#" and v[0] not in names:
                names.append(v[0])
        ops.append({"eng": eng, "outs": outs, "ins": ins, "subs": subs, "cost": cost, "kind": kind, "bytes": nbytes,
                    "banks": names, "after": list(needs), "lean": lean[0]})
        return len(ops) - 1

    def size(v):
        return v[2] - v[1]

    def narrow(*vs):
        return all(v[0][0] != "#" and BYTES[SCRATCH[v[0]][2]] == 2 for v in vs)

    def cyc(n):
        return max(64, n) * CYCLE

    def one(eng, outs, ins, call, cost):
        op(eng, outs, ins, [(outs, ins, call)], cost)

    def copy(o, i, e="vs"):
        n = size(o)
        cost = {"v": cyc(n * 0.5 if narrow(o, i) else n), "s": cyc(n)}
        one(e, [o], [i], lambda q, x: q.tensor_copy(o[3](), i[3]()) if x == "v" else q.activation(o[3](), i[3](), COPY), cost)

    def scaled(o, i, sc, b=None):
        if b is None:
            one("s", [o], [i, sc], lambda q, x: q.activation(o[3](), i[3](), COPY, scale=sc[3]()), {"s": cyc(size(o))})
        else:
            one("s", [o], [i, sc, b], lambda q, x: q.activation(o[3](), i[3](), IDENTITY, bias=b[3](), scale=sc[3]()),
                {"s": cyc(size(o))})

    def ts(o, i, s1, op0, s2=None, op1=None, n=None):
        rd = [i] + [s for s in (s1, s2) if isinstance(s, tuple)]

        def call(q, x):
            a1 = s1[3]() if isinstance(s1, tuple) else s1
            a2 = s2[3]() if isinstance(s2, tuple) else s2
            if op1 is None:
                return q.tensor_scalar(o[3](), i[3](), a1, None, op0)
            return q.tensor_scalar(o[3](), i[3](), a1, a2, op0, op1)
        one("v", [o], rd, call, {"v": cyc(size(i))})

    def tt(o, a, b, f):
        n = size(a) * (1 if a[0][0] == "#" or b[0][0] == "#" else 2)
        one("v", [o], [a, b], lambda q, x: q.tensor_tensor(o[3](), a[3](), b[3](), f), {"v": cyc(n)})

    def fill(o, c):
        one("v", [o], [], lambda q, x: q.memset(o[3](), c), {"v": cyc(size(o) * (0.5 if narrow(o) else 1))})

    def ind(w, l):
        return w[3]().indirect(l[3]())

    def pick(o, w, l, e="vs"):
        n = size(l) * 16 * GATHER * CYCLE
        one(e, [o], [w, l], lambda q, x: q.tensor_copy(o[3](), ind(w, l)) if x == "v" else q.activation(o[3](), ind(w, l), COPY),
            {"v": n + 0.05, "s": n + 0.065})

    def pick2(o, w, l, b, f):
        one("v", [o], [w, l, b], lambda q, x: q.tensor_tensor(o[3](), ind(w, l), b[3](), f),
            {"v": size(l) * 16 * GATHER * CYCLE + 0.05})

    def put(w, l, i):
        one("v", [w], [l, i], lambda q, x: q.tensor_copy(ind(w, l), i[3]()), {"v": size(l) * 16 * SCATTER * CYCLE + 0.05})

    def mms(items):
        outs, ins, subs, cost = [], [], [], 0.0
        for o, l, r, a, z in items:
            outs.append(o)
            ins += [l, r]
            subs.append(([o], [l, r], lambda q, x, o=o, l=l, r=r, a=a, z=z: q.matmul(o[3](), l[3](), r[3](), a, z)))
            cost += max(64, size(r)) * (1 if narrow(l) else 4) * PE * CYCLE
        op("t", outs, ins, subs, {"t": cost})

    def mm(o, l, r):
        mms([(o, l, r, True, True)])

    def iota(o, pattern, base, cm, small=False):
        if small:
            call = lambda q, x: q.iota(o[3](), pattern, base, cm, allow_small_or_imprecise_dtypes=True)
        else:
            call = lambda q, x: q.iota(o[3](), pattern, base, cm)
        one("g", [o], [], call, {"g": 0.13 + 2 * size(o) * CYCLE})

    def zeros(o):
        iota(o, [[0, size(o)]], 0, 0, True)

    def dmas(sem, items, nbytes, extra=()):
        e = items[0][0]
        outs, ins = [], list(extra)
        for _, o, i in items:
            outs += [o] if o[0] and o[:3] not in [x[:3] for x in outs] else []
            ins += [i] if i[0] else []
        op(e, outs, ins, (sem, items, list(extra)), {e: DMA_ISSUE * len(items)}, "dma", nbytes)

    def send(q, src, dst, sem):
        sent[sem, (q - me) % N] = op("g", [], [src], (q, src, dst, sem), {"g": ISSUE}, "send",
                                     128 * size(src) * BYTES[SCRATCH[src[0]][2]])

    def expect(buf, width, sem):
        for d in (1, 2, 3):
            q, s = (me - d) % N, "%s%d" % (sem, d)
            v = V(buf, q * width, (q + 1) * width)
            op("-", [v], [], (v, s, q), {}, "come", 0, [sent[sem, d]])

    ring = [(me + d) % N for d in (1, 2, 3, 0)]
    come = [(me - d) % N for d in (0, 1, 2, 3)]

    def U(t):
        return ("u" + t, 0, 32, lambda: T["u" + t][:, :, :])

    def table(t, e):
        dmas("dt" + t, [(e, V("t" + t), H(T[t][:, :]))], 16384)

    def table3(t, e):
        dmas("du" + t, [(e, U(t), H(T[t][:, :]))], 16384)

    table3("lc", "y")
    dmas("dfb", [("s", V("fb16", p0=0, p1=16), H(T.fb[:, :]))], 131072)
    dmas("dfe", [("y", V("fc16", p0=0, p1=16), H(T.fc[:, DC:4096]))], 65536)
    table3("lb", "s")
    dmas("dfc", [("y", group("fcr", b, 0, DC), H(T.fc[:, 0:DC])) for b in range(8)], 16 * DC * 2 * 8)
    table("la", "y")
    table("xa", "y")
    table3("la", "y")
    dmas("dv", [("y", V("v8", p0=0, p1=8), H(T.v[:, :]))], 16384)
    for t in ("xc", "xb", "ob", "lb"):
        table(t, "y")

    iota(V("Di"), [[-1, 128]], 128, 1)
    iota(V("k1"), [[0, 8]], 0, 1)
    iota(V("kri"), [[-32, 4]], 0, 1)
    iota(V("kgi"), [[-16, 8]], 0, 1)
    iota(V("trash"), [[16, 32]], 4097, 1, True)
    iota(V("w01"), [[1, 8]], 0, 0, True)
    iota(V("vsi", p1=8), [[1, 128]], 0, -16)
    iota(V("Gi"), [[-16, 8], [0, 16]], 0, 1)
    iota(V("a1"), [[128, 4], [0, 128]], 0, 0, True)
    iota(V("a2"), [[0, 4], [1, 128]], 8, 0, True)

    fill(V("X"), 0.0)
    ts(V("Ei"), V("Di"), 15, OP.bitwise_and)
    ts(V("hk"), V("k1"), 4, OP.arith_shift_right, 1, OP.bitwise_and)
    ts(V("p15"), V("k1"), 15, OP.bitwise_and)
    ts(V("krs"), V("kri"), 5, OP.arith_shift_right)
    ts(V("kgs"), V("kgi"), 4, OP.arith_shift_right)
    ts(V("E16"), V("Ei"), 0, OP.is_equal)
    ts(V("E"), V("Ei"), 0, OP.is_equal)
    ts(V("hf"), V("hk"), 1, OP.mult)
    ts(V("m0"), V("p15"), 0, OP.is_equal)
    ts(V("m1"), V("p15"), 1, OP.is_equal)
    ts(V("hb"), V("hf"), 512.0, OP.mult, V("m0", 0, 1), OP.mult)
    ts(V("rm4"), V("krs"), 0, OP.is_equal)
    ts(V("hm"), V("hk"), 0, OP.is_equal)
    for b in range(8):
        ts(V("X", 128 * (b % 4) + 16 * b, 128 * (b % 4) + 16 * b + 16), V("E", 0, 16),
           V("hm" if b < 4 else "hf", 0, 1), OP.mult)
    ts(V("rm8"), V("kgs"), 0, OP.is_equal)
    ts(V("n0"), V("p15"), 0, OP.not_equal)
    ts(V("N1"), V("Di"), 129, OP.is_equal, V("n0", 0, 1), OP.mult)
    ts(V("N2"), V("Di"), 113, OP.is_equal, V("m0", 0, 1), OP.mult)
    ts(V("ident"), V("Di"), 128, OP.is_equal)
    ts(V("rsel"), V("krs"), 0, OP.is_equal)
    ts(V("Gs"), V("Gi"), 4, OP.arith_shift_right)
    ts(V("GRP"), V("Gs"), 0, OP.is_equal)
    ts(V("vss", p1=8), V("vsi", p1=8), 4, OP.arith_shift_right)
    ts(V("vsel", p1=8), V("vss", p1=8), 0, OP.is_equal)

    def tiles_list(t, dst):
        tm, u = "tm" + t[1], U(t)
        for r in range(4):
            ts((tm, r, r + 1, lambda r=r: T[tm][:, :, r, :]), u, V("rm4", r, r + 1), OP.mult)
        p = bank()
        mms([(V(p, 0, 32), V("X", 128 * b, 128 * b + 128), (tm, 0, 4, lambda b=b: T[tm][:, b, :, :]), b == 0, b == 3)
             for b in range(4)])
        copy(V(dst), V(p, 0, 32), "v")

    tiles_list("lc", "Lc")
    tiles_list("lb", "Lb")
    for i in range(8):
        for src, dst, lo in (("fc16", "fcr", DC), ("fb16", "fbr", 0)):
            if 512 * i >= lo:
                p = bank()
                mm(V(p), V("E16", p1=16), V(src, 512 * i - lo, 512 * i - lo + 512, p1=16))
                copy(V(dst, 512 * i, 512 * i + 512), V(p))

    for r in ring:
        pick(V("CB", 256 * r, 256 * r + 128), V("fcr"), V("Lc", 8 * r, 8 * r + 8))
        pick(V("CB", 256 * r + 128, 256 * r + 256), V("fbr"), V("Lb", 8 * r, 8 * r + 8))
        if r != me:
            send(r, V("CB", 256 * r, 256 * r + 256), T["LCB"][:, 256 * me:256 * me + 256], "c")
    expect("LCB", 256, "c")
    for i in range(4):
        zeros(V("zA", 1026 * i, 1026 * i + 1026))

    dmas("dfa", [("y", group("far", b), H(T.fa[:, :])) for b in range(8)], 1 << 20, [V("LCB")])
    dmas("dfg", [("y", group("fag", b), H(T.fa[:, 512 * b:512 * b + 512])) for b in range(8)], 131072)

    for name in ("SELB", "SEL"):
        for b in range(8):
            scaled(V(name, 128 * b, 128 * b + 128), V("E"), V("rm8", b, b + 1))
    lean[0] = LEAN["ss"]
    scaled(V("s1"), V("a1"), V("m0", 0, 1), V("hb", 0, 1))
    scaled(V("s2"), V("a2"), V("m1", 0, 1))
    tt(V("ssrc"), V("s1"), V("s2"), OP.add)

    def places(t, dst, a, b, d, e):
        ts(V(a), V(t), 0x1F0, OP.bitwise_and)
        ts(V(b), V(t), 5, OP.arith_shift_right, 0x70, OP.bitwise_and)
        ts(V(d), V(t), 15, OP.bitwise_and)
        ts(V(a), V(a), 8, OP.mult)
        tt(V(b), V(a), V(b), OP.add)
        tt(V(e), V(b), V(d), OP.add)
        copy(V(dst), V(e), "v")

    def runs(yl, sn, tr, snu, off, fl):
        p = bank()
        mms([(V(p, 0, 32), V("N1"), V(yl, 0, 32), True, False), (V(p, 0, 32), V("N2"), V(yl, 1, 33), False, True)])
        tt(V(sn), V(p, 0, 32), V(yl, 0, 32), OP.is_equal)
        copy(V(snu), V(sn), "v")
        tt(V(tr), V(sn), V("trash"), OP.mult)
        tt(V(tr), V(tr), V(yl, 0, 32), OP.max)
        copy(V(off), V(tr), "v")
        fill(V(fl, 0, 8), 0.0)
        pick(V(fl, 8, 520), V("w01"), V(snu))

    def lists(src, col, dst):
        p = bank()
        mms([(V(p, 4 * k, 4 * k + 4), V(src, 128 * col[k], 128 * col[k] + 128), V("rsel"), True, True) for k in range(32)])
        for r in range(4):
            copy(V(dst, 32 * r, 32 * r + 32), V(p, r, 128, 4), "v")

    lean[0] = LEAN["vex"]
    p = bank()
    mm(V(p), V("vsel", p1=8), V("v8", p1=8))
    copy(V("vex"), V(p))
    lean[0] = LEAN["list"]
    fill(V("yl"), 0.0)
    ts(V("yl", 0, 32), V("txa"), 1, OP.add)
    runs("yl", "sa", "ta", "snA", "offA", "flA")
    lean[0] = LEAN["jc"]
    copy(V("jc"), V("txc"), "v")
    copy(V("jb"), V("txb"), "v")
    lean[0] = LEAN["fas"]
    tiles_list("la", "La")
    lean[0] = LEAN["inv"]
    places("tla", "pia", "ba", "bb", "bd", "pii")
    copy(V("pif"), V("pii"), "v")
    lean[0] = LEAN["wf"]
    for i in range(4):
        fill(V("W", 1024 * i, 1024 * i + 1024), 0.0)
    lean[0] = LEAN["inv"]
    put(V("W"), V("pia"), V("ssrc"))
    p = bank()
    mms([(V(p, 32 * i, 32 * i + 32), V("SEL", 128 * i, 128 * i + 128), V("pif"), True, True) for i in range(8)])
    for k in range(8):
        copy(V("Lr", 32 * k, 32 * k + 32), V(p, k, 256, 8), "v")
    lean[0] = LEAN["r"]
    for i in range(8):
        pick(V("R", 512 * i, 512 * i + 512), V("W"), V("Lr", 32 * i, 32 * i + 32), "s")
    lists("R", [(i % 8) * 4 + i // 8 for i in range(32)], "idx")
    lean[0] = LEAN["ya"]
    lists("W", list(range(32)), "inva")
    lean[0] = 0.0

    for n, q in enumerate(come):
        buf = "CB" if q == me else "LCB"
        for f, win in ((0, "Cw"), (1, "Bw")):
            for h in range(2):
                p = bank()
                mms([(V(p, 128 * b, 128 * b + 128), V("SELB", 128 * (4 * h + b), 128 * (4 * h + b) + 128),
                      V(buf, 256 * q + 128 * f, 256 * q + 128 * f + 128), True, True) for b in range(4)])
                copy(V(win, 1024 * q + 512 * h, 1024 * q + 512 * h + 512), V(p))
    pick2(V("vc"), V("Cw"), V("jc"), V("vex"), OP.mult)
    pick2(V("w1"), V("Bw"), V("jb"), V("vc"), OP.mult)

    def addruns(src, fl, off, z, scn):
        o, a, b = V(scn), V(fl, 7, 519), V(src)
        one("v", [o], [a, b], lambda q, x: q.tensor_tensor_scan(o[3](), a[3](), b[3](), 0.0, OP.mult, OP.add), {"v": cyc(512)})
        put(V(z), V(off), V(scn))

    def reduce(z, land, sem, RT, PT, pw):
        lean[0] = LEAN["red"]
        for q in ring[:3]:
            p = bank()
            mms([(V(p, 16 * b, 16 * b + 16), V(z, 1 + 1024 * q + 128 * b, 129 + 1024 * q + 128 * b), V("E", 0, 16), True, True)
                 for b in range(8)])
            copy(V(RT, 128 * q, 128 * q + 128), V(p, 0, 128))
            p = bank()
            o, i, idn = V(p, 0, 128), V(RT, 128 * q, 128 * q + 128), V("ident")
            op("t", [o], [i, idn], [([o], [i, idn], lambda k, x, o=o, i=i: k.transpose(o[3](), i[3](), idn[3]()))],
               {"t": 512 * PE * CYCLE})
            copy(V(PT, 128 * q, 128 * q + 128), V(p, 0, 128))
            send(q, V(PT, 128 * q, 128 * q + 128), T[land][:, 128 * me:128 * me + 128], sem)
        lean[0] = LEAN["pw"]
        for h in range(4):
            p = bank()
            c = 1 + 1024 * me + 256 * h
            mm(V(p, 0, 256), V("E"), V(z, c, c + 256))
            copy(V(pw, 8 + 256 * h, 264 + 256 * h), V(p, 0, 256))
        lean[0] = 0.0
        expect(land, 128, sem)

    def spread(buf, q, win, at, parts):
        w = 8 // parts
        for h in range(parts):
            p = bank()
            mms([(V(p, 128 * b, 128 * b + 128), V("SEL", 128 * (w * h + b), 128 * (w * h + b) + 128),
                  V(buf, 128 * q, 128 * q + 128), True, True) for b in range(w)])
            copy(V(win, at + 128 * w * h, at + 128 * w * (h + 1)), V(p, 0, 128 * w))

    addruns("w1", "flA", "offA", "zA", "scn")
    zeros(V("fcr", 0, 2048))
    reduce("zA", "LP", "p", "RT", "PT", "pw%d" % me)

    def gather(q, lst, o, prev, own="pw%d" % me):
        w, l = V(own if q == me else "pw%d" % q), V(lst, 32 * q, 32 * q + 32)
        if prev is None:
            pick(V(o), w, l)
        else:
            pick2(V(o), w, l, V(prev), OP.add)

    zeros(V("fcr", 2048, 4096))
    zeros(V("zB", 0, 2048))
    for name in ("qw", "pw0", "pw1", "pw2", "pw3"):
        fill(V(name, 0, 8), 0.0)
    gather(me, "idx", "ac0", None)
    lean[0] = LEAN["fas"]
    pick(V("faS"), V("far"), V("La"))
    lean[0] = 0.0
    for n in (1, 2):
        spread("LP", come[n], "pw%d" % come[n], 8, 4)
        gather(come[n], "idx", "ac%d" % n, "ac%d" % (n - 1))
    q = come[3]
    spread("LP", q, "pw%d" % q, 8, 8)
    for r in ring[:OWN] + [me] + ring[OWN:3]:
        lo, hi = 128 * r, 128 * r + 128
        lean[0] = LEAN["own"] if r == me else 0.0
        pick2(V("ac3", lo, hi), V("pw%d" % q), V("idx", 32 * q + 8 * r, 32 * q + 8 * r + 8), V("ac2", lo, hi), OP.add)
        tt(V("OT", lo, hi), V("ac3", lo, hi), V("faS", lo, hi), OP.mult)
        if r != me:
            send(r, V("OT", lo, hi), T["LA"][:, 128 * me:128 * me + 128], "n")
    lean[0] = 0.0
    expect("LA", 128, "n")
    zeros(V("zB", 2048, 4104))

    lean[0] = LEAN["lb"]
    ts(V("nb"), V("txb"), 4096, OP.mult)
    tt(V("nbi"), V("nb"), V("txa"), OP.add)
    for k in range(16):
        ts(("xe", k, k + 1, lambda k=k: T["xe"][:, k:512:16]), V("nbi"), V("E", k, k + 1), OP.mult)
    p = bank()
    mm(V(p), V("GRP"), V("xe"))
    copy(V("xr"), V(p))
    copy(V("jo"), V("tob"), "v")
    for i in range(4):
        pick2(V("mk", 128 * i, 128 * i + 128), V("xr"), V("jo", 8 * i, 8 * i + 8), V("E"), OP.mult)
    tt(V("m2"), V("mk", 0, 512, 2), V("mk", 1, 512, 2), OP.add)
    tt(V("m3"), V("m2", 0, 256, 2), V("m2", 1, 256, 2), OP.add)
    tt(V("m4"), V("m3", 0, 128, 2), V("m3", 1, 128, 2), OP.add)
    tt(V("nhi"), V("m4", 0, 64, 2), V("m4", 1, 64, 2), OP.add)
    ts(V("nlo"), V("nhi"), 4095, OP.bitwise_and)
    copy(V("ja"), V("nlo"), "v")
    ts(V("nhi"), V("nhi"), 12, OP.arith_shift_right)
    fill(V("ym"), 0.0)
    ts(V("ym", 0, 32), V("nhi"), 1, OP.add)
    runs("ym", "sb", "tb", "snB", "offB", "flB")
    lean[0] = LEAN["vco"]
    pick(V("vco"), V("vc"), V("jo"))
    lean[0] = LEAN["ib"]
    places("tlb", "pib", "be", "bf", "bg", "pij")
    put(V("fcr"), V("pib"), V("ssrc"))
    lists("fcr", list(range(32)), "invb")

    lean[0] = LEAN["ya"]
    gather(me, "inva", "ya0", None)
    for n in (1, 2, 3):
        gather(come[n], "inva", "ya%d" % n, "ya%d" % (n - 1))
    tt(V("yo"), V("ya3"), V("fag"), OP.mult)
    dmas("dya", [("y", H(T.ya[:, 512 * b:512 * b + 512]), group("yo", b)) for b in range(8)], 262144)
    lean[0] = 0.0

    spread("OT", me, "Aw", 1024 * me, 4)
    for n in (1, 2, 3):
        spread("LA", come[n], "Aw", 1024 * come[n], 4)
    pick2(V("w2"), V("Aw"), V("ja"), V("vco"), OP.mult)
    addruns("w2", "flB", "offB", "zB", "scm")
    reduce("zB", "LQ", "q", "RU", "PU", "qw")

    gather(me, "invb", "ac0", None, "qw")
    for n in (1, 2, 3):
        q = come[n]
        spread("LQ", q, "pw%d" % q, 8, 4)
        gather(q, "invb", "ac%d" % n, "ac%d" % (n - 1))
    dmas("dyb", [("ys"[b % 2], H(T.yb[:, 512 * b:512 * b + 512]), group("ac3", b)) for b in range(8)], 262144)

    for i, e, at in order(ops):
        where.update(at)
        o = ops[i]
        if o["kind"] == "c":
            for outs, ins, call in o["subs"]:
                emit(e, outs, ins, call)
        elif o["kind"] == "dma":
            emit_dmas(*o["subs"])
        elif o["kind"] == "send":
            emit_send(*o["subs"])
        else:
            emit_come(*o["subs"])
    for sem, n in count.items():
        if waited.get(sem, 0) < n:
            g.wait_ge(T.sem[sem], n)
